import numpy as np, ml_dtypes
CORES = [89,94,345,350]
N = 4
V, K, ROUNDS = 4096, 4, 3
CAPP = 256
def entries(a): return a.T.reshape(-1)
def pack(v, P): return np.ascontiguousarray(np.asarray(v, np.int32).reshape(-1, P).T)
def lists(rng, how):
    T = V * K; me = np.arange(N)[:, None]
    O = np.broadcast_to(me, (N, T)).copy()
    for r in range(N):
        p = rng.permutation(T); a = 0
        if how == "clump": p = (CAPP * int(rng.integers(T // CAPP)) + np.arange(T)) % T
        if how == "clump" and r % 2: p = 16 * (p % (T // 16)) + p // (T // 16)
        for o in range(N):
            if o != r: c = CAPP if how in ("clump", "full") else int(rng.integers(0, CAPP + 1)); O[r, p[a:a + c]] = o; a += c
    I = V * O + rng.integers(0, V, (N, T))
    if how == "alike": I = V * O + rng.integers(0, V, N)[O]
    if how == "edge": I = V * O + np.where(rng.random((N, T)) < 0.5, 0, V - 1)
    if how == "line": I = np.minimum(V * me + np.arange(T)[None, :] // K + 1, N * V - 1)
    return {"nb": np.stack([pack(i, 16) for i in I])}
def setup_inputs(rng):
    return dict({"x": rng.standard_normal((N, 128, V), dtype=np.float32).astype(ml_dtypes.bfloat16)}, **lists(rng, "uniform"))
def setup_inputs_alike(rng):
    d = setup_inputs(rng); d.update(lists(rng, "alike"))
    for k in ("x",): d[k] = (d[k].astype(np.float32) * 1048576.0).astype(d[k].dtype)
    return d
def setup_inputs_clump(rng):
    d = setup_inputs(rng); d.update(lists(rng, "clump"))
    for k in ("x",): d[k] = (d[k].astype(np.float32) * (1 / 1024.0)).astype(d[k].dtype)
    return d
def setup_inputs_edge(rng):
    d = setup_inputs(rng); d.update(lists(rng, "edge"))
    return d
def setup_inputs_full(rng):
    d = setup_inputs(rng); d.update(lists(rng, "full"))
    return d
def setup_inputs_line(rng):
    d = setup_inputs(rng); d.update(lists(rng, "line"))
    return d
def check_inputs(x):
    bad = []
    if x["nb"].min() < 0 or x["nb"].max() >= N * V: bad.append("nb out of range")
    if np.abs(x["x"].astype(np.float32)).max() > 1e30: bad.append("x beyond -1e30 to 1e30")
    for r in range(N):
        c = np.bincount(entries(x["nb"][r]) // V, minlength=N); c[r] = 0
        if int(c.max()) > CAPP: bad.append("more than CAPP entries of a list point into one other rank's part")
    return bad
def reference(x, nb):
    A = np.concatenate(list(x), axis=1)
    NB = np.concatenate([entries(a) for a in nb]).reshape(N * V, K)
    for k in range(ROUNDS):
        B = A.copy()
        for j in range(K): B = np.maximum(B, A[:, NB[:, j]])
        A = B
    return {"y": np.stack([A[:, V * r:V * r + V] for r in range(N)])}

@@ -1,0 +1,489 @@
+from concourse.bass import DstId, RemoteDMATransfer
+from concourse.mybir import AluOpType, ActivationFunctionType
+
+NW = 4864
+SCRATCH = {"xs": ("dram", [4, 128, 1024], "bfloat16")}
+for _n, _w, _d in (("W0", NW, "bfloat16"), ("W1", NW, "bfloat16"), ("W2", NW, "bfloat16"), ("R3", 1024, "bfloat16"),
+                   ("YL", 4096, "bfloat16"), ("RL", 576, "bfloat16"), ("QS", 576, "bfloat16"), ("FW", 384, "bfloat16"),
+                   ("FP", 24, "uint16"), ("LQ", 72, "uint16"), ("PB", 24, "uint16"), ("LM", 256, "uint16"),
+                   ("TAB", 256, "float32"), ("TG", 1024, "float32"), ("GA", 4096, "bfloat16"), ("SC", 4096, "bfloat16"),
+                   ("GQ", 960, "bfloat16"), ("SQ", 960, "bfloat16"), ("MM", 1280, "bfloat16"), ("MQ", 960, "bfloat16"),
+                   ("S8", 1024, "float32"), ("S2", 256, "float32"), ("RB", 512, "bfloat16"), ("IS", 256, "bfloat16"),
+                   ("TRI", 128, "bfloat16"), ("DM", 128, "bfloat16"), ("SH", 128, "bfloat16"), ("TB", 4, "bfloat16"),
+                   ("RT", 640, "bfloat16"), ("DS", 644, "bfloat16"), ("CP", 768, "bfloat16"), ("SEG", 384, "float32"),
+                   ("FF", 512, "float32"), ("CC", 384, "float32"), ("EE", 768, "float32"), ("EV", 768, "float32"),
+                   ("JK", 768, "float32"), ("TT", 384, "float32"), ("UU", 384, "float32"), ("REP", 128, "float32"),
+                   ("ROW", 128, "float32"), ("NBI", 128, "int32"), ("VI", 128, "int32")):
+    SCRATCH[_n] = ("sbuf", [128, _w], _d)
+for _k in range(8):
+    SCRATCH["P%d" % _k] = ("psum", [128, 512], "float32")
+PACK = {}
+for _b, _d, _l in (("PU", "uint16", "OFP 12 CU 12 AU 12 CL 48"),
+                   ("PN", "int32", "CI 12 C2 12 A2 12 PI 1 PC 8 OWN 128 LO 128 HI 128 VQ 12 OI 12 OJ 12 VR 128 VS 128"),
+                   ("PX", "float32", "NB 192 NM 192 R2A 192 R2B 192 CA 48 CM 48 CY 48 CZ 48 CO 48 PF 8 R16 16 KC 1 KC2 1 RC 1 "
+                    "H1 1 H2 1 H3 1 HM 16 M8 8 M4 4 SCOL 2 VC 6 RW 48 BC 3 R1 128 R4 128 LV 128 LR 128")):
+    _l, _o = _l.split(), 0
+    for _k in range(0, len(_l), 2):
+        PACK[_l[_k]] = (_b, _o, int(_l[_k + 1]))
+        _o += (int(_l[_k + 1]) + 7) // 8 * 8
+    SCRATCH[_b] = ("sbuf", [128, _o], _d)
+SEMAPHORES = ("v s p gi ls dn dx do dw0 dw1 dw2 dy ax at aq ar0 ar1 ar2 rq rr0 rr1 rr2".split()
+              + ["ay%d%d" % (q, c) for q in range(4) for c in range(2)])
+BIG = 9.99e29
+
+
+def bits(m):
+    return [1 << e for e in range(16) if m >> e & 1]
+
+
+def places(T, topo):
+    near = lambda a, b: topo.host(a) == topo.host(b) and topo.chip(a) == topo.chip(b)
+    world = range(512)
+    teams = [[c for c in world if near(c, k) and topo.die(c) == topo.die(k)] for k in T.cores]
+    relay = {}
+    for t in teams:
+        for s in t:
+            here = [c for c in world if near(c, s)]
+            there = [c for c in world if topo.same_plane(s, c) and topo.chip(c) == topo.chip(s)]
+            relay[s] = there[here.index(s)]
+    return teams, relay
+
+
+def others(r):
+    return [o for o in range(4) if o != r]
+
+
+_cache = {}
+
+
+def rank_program(g, core, T, topo):
+    if "p" not in _cache:
+        _cache["p"] = places(T, topo)
+    teams, relay = _cache["p"]
+    for r in range(4):
+        if core in teams[r]:
+            return team_program(g, core, T, topo, teams, relay, r, teams[r].index(core))
+    for s in relay:
+        if relay[s] == core:
+            return relay_program(g, core, T, topo, teams, s)
+
+
+def dst(topo, d, core):
+    rid, pid = topo.addr(d, core)
+    return DstId(rid=rid, pnc=pid)
+
+
+def cross(teams, topo, r):
+    return [o for o in others(r) if topo.host(teams[o][0]) != topo.host(teams[r][0])]
+
+
+def relay_program(g, core, T, topo, teams, s):
+    r = [k for k in range(4) if s in teams[k]][0]
+    q, far, n = teams[r].index(s), cross(teams, topo, r), 0
+    e = bits(topo.mask(core, teams[far[0]][q]))
+    if s == T.cores[r]:
+        g.wait_ge(T.sem["rq"], 8)
+        tr = []
+        for h, o in enumerate(far):
+            ri = others(o).index(r)
+            tr.append(RemoteDMATransfer(dst_ids=[dst(topo, d, core) for d in teams[o]], srcs=[T.FP[:]],
+                                        dsts=[T.LQ[:, 24 * ri:24 * ri + 24] for d in teams[o]],
+                                        dma_engine_mask=sum(e[4 * h:4 * h + 4]), remote_sem=T.sem["aq"]))
+        g.remote_dma_fused(tr, local_sem=T.sem["ls"])
+        n += 8
+    for k in range(3):
+        g.wait_ge(T.sem["rr%d" % k], 8)
+        tr = []
+        for h, o in enumerate(far):
+            c, f = 192 * k + 64 * others(o).index(r), 128 * k + 64 * h
+            tr.append(RemoteDMATransfer(dst_ids=[dst(topo, teams[o][q], core)], srcs=[T.FW[:, f:f + 64]],
+                                        dsts=[T.RL[:, c:c + 64]],
+                                        dma_engine_mask=sum(e[4 * h:4 * h + 4]), remote_sem=T.sem["ar%d" % k]))
+        g.remote_dma_fused(tr, local_sem=T.sem["ls"])
+        n += 8
+    g.wait_ge(T.sem["ls"], n)
+
+
+def team_program(g, core, T, topo, teams, relay, r, q):
+    home = T.cores[r]
+    isr = core == home
+    oth, far = others(r), cross(teams, topo, r)
+    mate = [o for o in oth if o not in far][0]
+    en_on, en_off = bits(topo.mask(core, teams[mate][q])), bits(topo.mask(core, relay[core]))
+    en_hi = [b for b in en_on if b not in en_off]
+    A, S = AluOpType, T.sem
+    COPY = ActivationFunctionType.Copy
+    queue = {"v": g.vector, "s": g.scalar, "p": g.tensor, "g": g, "y": g.sync}
+    n, seen = {}, {}
+
+    def u(name, a=0, b=None, p=slice(0, 128), step=1):
+        buf, o, w = PACK[name]
+        return T[buf][p, o + a:o + (w if b is None else b):step]
+
+    def wait(k, sem, val=None):
+        val = n.get(sem, 0) if val is None else val
+        if seen.get((k, sem), 0) < val:
+            queue[k].wait_ge(S[sem], val)
+            seen[(k, sem)] = val
+
+    def inc(ins, sem, c):
+        ins.then_inc(S[sem], c)
+        n[sem] = n.get(sem, 0) + c
+        return n[sem]
+
+    def V(f, *a, free=False):
+        if not free:
+            wait("v", "v")
+        return inc(f(*a), "v", 1)
+
+    ts, tt, cp, fill = g.vector.tensor_scalar, g.vector.tensor_tensor, g.vector.tensor_copy, g.vector.memset
+    scan = g.vector.tensor_tensor_scan
+
+    def act(out, in_, acc=None, free=False):
+        if not free:
+            wait("s", "s")
+        if acc is None:
+            return inc(g.scalar.activation(out, in_, COPY), "s", 1)
+        return inc(g.scalar.activation(out, in_, COPY, accum_out=acc), "s", 1)
+
+    def mm(out, l, rh, st=True, sp=True):
+        return inc(g.tensor.matmul(out, l, rh, st, sp), "p", 1)
+
+    def iota(out, pat, cm=0):
+        if cm:
+            return inc(g.iota(out, pat, 0, cm), "gi", 1)
+        return inc(g.iota(out, pat, 0, 0, allow_small_or_imprecise_dtypes=True), "gi", 1)
+
+    def select(buf, pat, base, cm, op, fillv=0.0):
+        return inc(g.affine_select(buf, buf, pat, op, fillv, base, cm), "gi", 1)
+
+    def rotate(W, c0, c1, sem):
+        for k in (1, 2, 3):
+            a = 32 * k
+            inc(g.sync.dma_start(W[0:128 - a, 1024 * k + c0:1024 * k + c1], W[a:128, c0:c1]), sem, 16)
+            inc(g.sync.dma_start(W[128 - a:128, 1024 * k + c0:1024 * k + c1], W[0:a, c0:c1]), sem, 16)
+
+    W = [T.W0, T.W1, T.W2, T.R3]
+    PS = [T["P%d" % k] for k in range(8)]
+    if isr:
+        inc(g.sync.dma_start(T.NBI[:], T.nb[:]), "dn", 16)
+        for b in range(4):
+            inc(g.sync.dma_start(T.xs[:, 32 * b:32 * b + 32, :], T.x[:, 1024 * b:1024 * b + 1024]), "dx", 16)
+        for b in range(4):
+            inc(g.scalar.dma_start(T.W0[32 * b:32 * b + 32, 0:1024], T.x[32 * q:32 * q + 32, 1024 * b:1024 * b + 1024]),
+                "do", 16)
+    iota(u("PI"), [[0, 1]], 1)
+    iota(u("R16"), [[1, 16]])
+    iota(T.ROW[:], [[0, 8], [1, 16]])
+    if isr:
+        iota(T.IS[:], [[1, 256]])
+        for b in (T.TRI[:], T.SH[:], T.DM[:]):
+            v0 = V(fill, b, 1.0, free=True)
+        V(fill, T.SEG[:], 1.0)
+        V(fill, T.SEG[:, 0:384:128], 0.0)
+    gc1 = n["gi"]
+    for b in (T.S8[:], T.S2[:], T.RB[:]):
+        vf = V(fill, b, 1.0, free=True)
+    pf = lambda c: u("PF", c, c + 1)
+
+    def small_constants():
+        for c, (sh, am) in enumerate([(5, 3), (4, 7), (0, 15), (2, 3), (4, 1), (0, 3), (0, 127), (1, 3)]):
+            V(ts, u("PC", c, c + 1), u("PI"), sh, am, A.logical_shift_right, A.bitwise_and, free=c > 0)
+        V(cp, u("PF"), u("PC"))
+        V(ts, u("SCOL", 0, 1), pf(6), 1.0, None, A.add)
+        V(ts, u("SCOL", 1, 2), pf(6), 129.0, None, A.add, free=True)
+        V(ts, u("KC"), pf(0), 1024.0, None, A.mult, free=True)
+        V(ts, u("KC2"), pf(0), -1024.0, 4096.0, A.mult, A.add, free=True)
+        V(ts, u("RC"), pf(7), -1024.0, 4096.0, A.mult, A.add, free=True)
+        V(ts, u("H1"), pf(0), 4.0, pf(5), A.mult, A.add, free=True)
+        V(ts, u("H2"), pf(4), -100.0, None, A.mult, free=True)
+        V(ts, u("M8"), u("R16", 0, 8), pf(1), None, A.is_equal, free=True)
+        V(ts, u("M4"), u("R16", 0, 4), pf(3), None, A.is_equal, free=True)
+        V(ts, T.REP[:], T.ROW[:], pf(2), None, A.is_equal, free=True)
+        V(tt, u("H3"), u("H1"), u("H2"), A.add)
+        V(ts, u("HM"), u("R16"), u("H3"), None, A.is_equal)
+
+    def late_fills():
+        for b, c in ((T.MM[:], BIG), (T.MQ[:], BIG), (u("R2A"), 0.0), (u("R2B"), 0.0)):
+            V(fill, b, c, free=True)
+        V(fill, T.MM[:, 0:1280:4], -BIG)
+        V(fill, T.MQ[:, 0:960:5], -BIG, free=True)
+
+    def selectors():
+        wait("g", "v", vf)
+        select(T.S2[:, 0:128], [[-2, 4], [0, 2], [-8, 16]], 0, 1, A.is_equal)
+        select(T.S2[:, 128:256], [[-2, 4], [0, 2], [-8, 16]], -1, 1, A.is_equal)
+        select(T.S8[:], [[-1, 8], [0, 8], [-8, 16]], 0, 1, A.is_equal)
+        select(T.RB[:], [[-32, 4], [0, 4], [-1, 32]], 0, 1, A.is_equal)
+
+    wait("v", "gi", gc1)
+    if isr:
+        wait("g", "gi", gc1)
+        wait("g", "v", v0)
+        select(T.TRI[:], [[1, 128]], 0, -1, A.is_gt)
+        select(T.SH[:], [[1, 128]], -1, -1, A.is_equal)
+        select(T.DM[:], [[1, 128]], 0, -1, A.is_equal)
+        wait("g", "gi")
+        gtri = select(T.DM[:], [[1, 128]], -1, -1, A.not_equal, -1.0)
+        wait("g", "gi")
+        wait("g", "dx")
+        tr = []
+        helpers = [c for c in teams[r] if c != core]
+        for h, c in enumerate(helpers):
+            tr.append(RemoteDMATransfer(dst_ids=[dst(topo, c, core)], srcs=[T.xs[teams[r].index(c)]], dsts=[T.W0[:, 0:1024]],
+                                        dma_engine_mask=sum(en_on[4 * h:4 * h + 4]), remote_sem=S["ax"]))
+        g.remote_dma_fused(tr, local_sem=S["ls"])
+        n["ls"] = n.get("ls", 0) + 12
+        selectors()
+        wait("y", "do")
+        rotate(T.W0, 0, 1024, "dw0")
+        wait("v", "dn")
+        V(ts, u("OWN"), T.NBI[:], 12, None, A.logical_shift_right)
+        V(ts, T.VI[:], T.NBI[:], 4095, None, A.bitwise_and, free=True)
+        for i, o in enumerate(oth + [r]):
+            V(ts, T.FF[:, 128 * i:128 * i + 128], u("OWN"), float(o), None, A.is_equal, free=i > 0)
+        V(scan, T.CC[:], T.SEG[:], T.FF[:, 0:384], 0.0, A.mult, A.add)
+        vt = V(cp, T.TB[:, 0:3], T.CC[:, 127:384:128])
+        wait("p", "v", vt)
+        wait("p", "gi", gtri)
+        pbase = mm(PS[3][:, 0:3], T.TRI[:], T.TB[:, 0:3])
+        V(tt, T.RT[:, 0:384], T.CC[:], T.FF[:, 0:384], A.mult)
+        V(ts, u("HI"), T.VI[:], 4032, None, A.bitwise_and, free=True)
+        V(ts, u("LO"), T.VI[:], 63, None, A.bitwise_and, free=True)
+        V(cp, T.RT[:, 384:512], u("HI"))
+        vr = V(cp, T.RT[:, 512:640], u("LO"), free=True)
+        wait("p", "v", vr)
+        wait("p", "p")
+        mm(PS[4][:, 0:384], T.DM[:], T.RT[:, 0:384])
+        mm(PS[5][:, 0:256], T.DM[:], T.RT[:, 384:640])
+        pd = mm(PS[5][:, 256:259], T.SH[:], T.TB[:, 0:3])
+        wait("s", "p", pd)
+        act(T.DS[:, 0:384], PS[4][:, 0:384])
+        sd = act(T.DS[:, 384:643], PS[5][:, 0:259], free=True)
+        wait("v", "p", pbase)
+        for i in range(3):
+            vcp = V(ts, T.CP[:, 256 * i:256 * i + 256], T.IS[:], PS[3][:, i:i + 1], None, A.is_ge, free=i > 0)
+        small_constants()
+        wait("p", "v", vcp)
+        wait("p", "s", sd)
+        vev, ptl = {}, {}
+
+        def tile(t):
+            i, X, l = t // 2, PS[t % 3], T.CP[:, 128 * t:128 * t + 128]
+            wait("p", "p")
+            if t >= 3:
+                wait("p", "v", vev[t - 3])
+            mm(X[:, 0:128], l, T.DS[:, 128 * i:128 * i + 128])
+            mm(X[:, 128:256], l, T.DS[:, 384:512], True, False)
+            mm(X[:, 128:256], l, T.DS[:, 512:640], False, True)
+            ptl[t] = mm(X[:, 256:257], l, T.DS[:, 640 + i:641 + i])
+
+        for t in range(3):
+            tile(t)
+        for t in range(6):
+            X, c = PS[t % 3], slice(128 * t, 128 * t + 128)
+            wait("v", "p", ptl[t])
+            V(ts, T.EE[:, c], X[:, 0:128], X[:, 256:257], u("SCOL", t % 2, t % 2 + 1), A.add, A.is_equal)
+            vev[t] = V(tt, T.EV[:, c], T.EE[:, c], X[:, 128:256], A.mult)
+            if t + 3 < 6:
+                tile(t + 3)
+            wait("s", "v", vev[t])
+            sacc = act(T.JK[:, c], T.EV[:, c], u("VC", t, t + 1))
+        wait("v", "s", sacc)
+        for t in range(6):
+            i, h = t // 2, t % 2
+            for kk in range(2):
+                a = 12 * (2 * h + kk) + 4 * i
+                vw = V(ts, u("RW", a, a + 4), u("M8", 4 * kk, 4 * kk + 4), u("VC", t, t + 1), None, A.mult, free=t + kk > 0)
+        wait("p", "v", vw)
+        wait("p", "p")
+        pw = mm(PS[6][:, 0:48], T.REP[:], u("RW"))
+        wait("v", "p", pw)
+        for k in range(4):
+            p = slice(32 * k, 32 * k + 32)
+            V(cp, u("VQ", p=p), PS[6][p, 12 * k:12 * k + 12], free=k > 0)
+        V(ts, u("OI"), u("VQ"), u("KC2"), None, A.add)
+        V(ts, u("OJ"), u("OI"), 4095, None, A.bitwise_and)
+        V(cp, T.PB[:, 0:12], u("OJ"))
+        vpb = V(cp, T.PB[:, 12:24], u("VQ"), free=True)
+        wait("g", "v", vpb)
+        ri = others(mate).index(r)
+        g.remote_dma_fused([
+            RemoteDMATransfer(dst_ids=[dst(topo, relay[core], core)], srcs=[T.PB[:]], dsts=[T.FP[:]],
+                              dma_engine_mask=sum(en_off), remote_sem=S["rq"]),
+            RemoteDMATransfer(dst_ids=[dst(topo, d, core) for d in teams[mate]], srcs=[T.PB[:]],
+                              dsts=[T.LQ[:, 24 * ri:24 * ri + 24] for d in teams[mate]],
+                              dma_engine_mask=sum(en_hi), remote_sem=S["aq"])], local_sem=S["ls"])
+        n["ls"] += 16
+        for i in range(3):
+            V(ts, u("BC", i, i + 1), PS[3][:, i:i + 1], 4095.0 + 256 * i, None, A.add, free=i > 0)
+        for i in range(3):
+            c = slice(128 * i, 128 * i + 128)
+            V(ts, T.TT[:, c], T.FF[:, c], u("BC", i, i + 1), None, A.mult, free=i > 0)
+        V(ts, u("VS"), T.VI[:], u("RC"), None, A.add, free=True)
+        V(tt, u("LV"), T.FF[:, 384:512], T.VI[:], A.mult, free=True)
+        V(tt, T.UU[:], T.TT[:], T.RT[:, 0:384], A.add)
+        V(ts, u("VR"), u("VS"), 4095, None, A.bitwise_and, free=True)
+        V(tt, u("R1"), T.UU[:, 0:128], T.UU[:, 128:256], A.add)
+        V(tt, u("LR"), T.FF[:, 384:512], u("VR"), A.mult, free=True)
+        V(tt, u("R4"), u("R1"), T.UU[:, 256:384], A.add)
+        V(tt, T.TAB[:, 0:128], u("R4"), u("LV"), A.add)
+        vtab = V(tt, T.TAB[:, 128:256], u("R4"), u("LR"), A.add, free=True)
+        wait("g", "v", vtab)
+        g.remote_dma_fused([
+            RemoteDMATransfer(dst_ids=[dst(topo, c, core) for c in helpers], srcs=[T.TAB[:]], dsts=[T.TAB[:] for c in helpers],
+                              dma_engine_mask=sum(en_on), remote_sem=S["at"])], local_sem=S["ls"])
+        n["ls"] += 16
+        wait("p", "v", vtab)
+        wait("v", "v")
+    else:
+        wait("v", "v")
+        small_constants()
+        selectors()
+        n["ax"], n["at"] = 4, 16
+        wait("y", "ax")
+        rotate(T.W0, 0, 1024, "dw0")
+        wait("p", "v")
+        wait("v", "v")
+        wait("p", "at")
+    late_fills()
+    wait("p", "gi")
+    wait("p", "s")
+    wait("p", "p")
+    mm(PS[6][:, 0:128], T.S2[:, 0:128], T.TAB[:, 128:256])
+    mm(PS[6][:, 128:256], T.S2[:, 128:256], T.TAB[:, 128:256])
+    for m in range(8):
+        pg = mm(PS[4 + m // 4][:, 128 * (m % 4):128 * (m % 4) + 128], T.S8[:, 128 * m:128 * m + 128], T.TAB[:, 0:128])
+    n["aq"] = 16
+    cols = [24 * ri + 4 * others(o).index(r) for ri, o in enumerate(oth)]
+    src = "do" if isr else "ax"
+    wait("s", "aq")
+    wait("s", "dw0")
+    wait("s", src)
+    for ri in range(3):
+        sq = act(T.QS[:, 64 * ri:64 * ri + 64], T.W0[:, 0:4096].indirect(T.LQ[:, cols[ri]:cols[ri] + 4]), free=True)
+
+    def send(k, sem, val):
+        wait("g", sem, val)
+        tr = []
+        for h, o in enumerate(far):
+            a, f = 192 * k + 64 * oth.index(o), 128 * k + 64 * h
+            tr.append(RemoteDMATransfer(dst_ids=[dst(topo, relay[core], core)], srcs=[T.QS[:, a:a + 64]],
+                                        dsts=[T.FW[:, f:f + 64]],
+                                        dma_engine_mask=sum(en_off[4 * h:4 * h + 4]), remote_sem=S["rr%d" % k]))
+        a, c = 192 * k + 64 * oth.index(mate), 192 * k + 64 * others(mate).index(r)
+        tr.append(RemoteDMATransfer(dst_ids=[dst(topo, teams[mate][q], core)], srcs=[T.QS[:, a:a + 64]],
+                                    dsts=[T.RL[:, c:c + 64]],
+                                    dma_engine_mask=sum(en_hi[0:4]), remote_sem=S["ar%d" % k]))
+        g.remote_dma_fused(tr, local_sem=S["ls"])
+        n["ls"] = n.get("ls", 0) + 12
+
+    send(0, "s", sq)
+    wait("v", "p", pg)
+    V(cp, T.LM[:], PS[6][:, 0:256])
+    V(cp, T.TG[:, 0:512], PS[4][:], free=True)
+    V(cp, T.TG[:, 512:1024], PS[5][:], free=True)
+    wait("v", "aq")
+    for ri in range(3):
+        V(cp, u("CI", 4 * ri, 4 * ri + 4), T.LQ[:, cols[ri] + 12:cols[ri] + 16], free=True)
+        V(cp, u("OFP", 4 * ri, 4 * ri + 4), T.LQ[:, cols[ri]:cols[ri] + 4], free=True)
+    V(ts, u("C2"), u("CI"), 2, None, A.logical_shift_right)
+    V(ts, u("A2"), u("CI"), 3, None, A.bitwise_and, free=True)
+    V(cp, u("CU"), u("C2"))
+    V(cp, u("AU"), u("A2"), free=True)
+    V(cp, u("NB"), T.TG[:].indirect(u("CU")))
+    vnm = V(tt, u("NM"), u("M4").indirect(u("AU")), u("NB"), A.mult)
+    wait("p", "v", vnm)
+    wait("p", "p")
+    lo96 = slice(0, 96)
+    mm(PS[7][lo96, 0:16], u("NM", 0, 96), u("HM"))
+    po = mm(PS[7][lo96, 16:32], u("NM", 96, 192), u("HM"))
+    wait("v", "p", po)
+    for t, R2 in enumerate(("R2A", "R2B")):
+        for c in range(6):
+            vr2 = V(ts, u(R2, 6 * t + c, 192, lo96, 12), PS[7][lo96, 16 * t:16 * t + 16], u("M8", c, c + 1, lo96), None, A.mult,
+                    free=t + c > 0)
+    wait("p", "v", vr2)
+    wait("p", "p")
+    mm(PS[6][:, 0:192], T.REP[lo96, :], u("R2A", p=lo96), True, False)
+    pc = mm(PS[6][:, 0:192], T.REP[lo96, :], u("R2B", p=lo96), False, True)
+    wait("v", "p", pc)
+    for b in range(4):
+        p = slice(32 * b, 32 * b + 32)
+        V(cp, u("CA", p=p), PS[6][p, 48 * b:48 * b + 48], free=b > 0)
+    V(ts, u("CM"), u("CA"), 4096.0, u("KC"), A.is_lt, A.mult)
+    V(tt, u("CY"), u("CA"), u("CM"), A.subtract)
+    V(ts, u("CZ"), u("CY"), 0.0, 4096.0, A.is_lt, A.mult)
+    V(tt, u("CO"), u("CY"), u("CZ"), A.add)
+    V(cp, u("CL"), u("CO"))
+    cuts = [0, 192, 512, 768, 928, 1024]
+    for k in range(3):
+        w, nxt = W[k], W[k + 1]
+        n["ar%d" % k] = 12
+        wait("p", "ar%d" % k)
+        wait("p", "v")
+        wait("p", "p")
+        for i in range(3):
+            for b in range(4):
+                c, a = 256 * i + 64 * b, 192 * k + 64 * i
+                pr = mm(PS[4 + c // 512][:, c % 512:c % 512 + 64], T.RB[:, 128 * b:128 * b + 128], T.RL[:, a:a + 64])
+        wait("s", "p", pr)
+        wait("v", "p", pr)
+        sr = act(w[:, 4096:4608], PS[4][:])
+        vr = V(cp, w[:, 4608:4864], PS[5][:, 0:256])
+        for e in ("v", "s"):
+            wait(e, "dw%d" % k)
+            if k == 0:
+                wait(e, src)
+        wait("s", "v", vr)
+        wait("v", "s", sr)
+        wait("s", "s")
+        win = w[:, 0:NW]
+        if k < 2:
+            for j in range(3):
+                V(cp, T.GQ[:, 1 + j:960:5], win.indirect(u("CL", 12 * j, 12 * j + 12)), free=j > 0)
+            act(T.GQ[:, 0:960:5], win.indirect(u("OFP")))
+            sq = act(T.GQ[:, 4:960:5], win.indirect(u("CL", 36, 48)), free=True)
+            wait("v", "s", sq)
+            V(scan, T.SQ[:], T.MQ[:], T.GQ[:], 0.0, A.min, A.max)
+            vq = V(cp, T.QS[:, 192 * k + 192:192 * k + 384], T.SQ[:, 4:960:5])
+            send(k + 1, "v", vq)
+        done = {}
+        for c in range(1, 5):
+            a, b = cuts[c], cuts[c + 1]
+            done[c] = act(T.GA[:, 4 * a:4 * b], win.indirect(T.LM[:, a // 4:b // 4]))
+        V(cp, T.GA[:, 0:4 * cuts[1]], win.indirect(T.LM[:, 0:cuts[1] // 4]))
+        for c in range(5):
+            a, b = cuts[c], cuts[c + 1]
+            if c:
+                wait("v", "s", done[c])
+            V(scan, T.SC[:, 4 * a:4 * b], T.MM[:, 0:4 * (b - a)], T.GA[:, 4 * a:4 * b], 0.0, A.min, A.max)
+            vm = V(tt, nxt[:, a:b], T.SC[:, 4 * a + 3:4 * b:4], w[:, a:b], A.max)
+            if b in (512, 1024):
+                h = b // 512 - 1
+                if k < 2:
+                    wait("y", "v", vm)
+                    rotate(nxt, 512 * h, b, "dw%d" % (k + 1))
+                elif isr:
+                    wait("y", "v", vm)
+                    for bb in range(4):
+                        inc(g.sync.dma_start(T.y[32 * q:32 * q + 32, 1024 * bb + 512 * h:1024 * bb + b],
+                                             nxt[32 * bb:32 * bb + 32, 512 * h:b]), "dy", 16)
+                else:
+                    wait("g", "v", vm)
+                    rid, pid = topo.addr(home, core)
+                    g.remote_dma(T.YL[:, 1024 * q + 512 * h:1024 * q + b], nxt[:, 512 * h:b], S["ay%d%d" % (q, h)], S["ls"],
+                                 pid, rid, topo.mask(core, home))
+                    n["ls"] += 16
+    if isr:
+        for h in range(2):
+            for c in helpers:
+                qq = teams[r].index(c)
+                n["ay%d%d" % (qq, h)] = 16
+                for bb in range(4):
+                    e, eng = (("y", g.sync), ("s", g.scalar))[bb % 2]
+                    wait(e, "ay%d%d" % (qq, h))
+                    inc(eng.dma_start(T.y[32 * qq:32 * qq + 32, 1024 * bb + 512 * h:1024 * bb + 512 * h + 512],
+                                      T.YL[32 * bb:32 * bb + 32, 1024 * qq + 512 * h:1024 * qq + 512 * h + 512]), "dy", 16)
+    for sem in n:
+        wait("g", sem)

@@ -2,33 +2,42 @@ from concourse.bass import DstId, RemoteDMATransfer
 from concourse.mybir import AluOpType, ActivationFunctionType
 
 NW = 4864
-SCRATCH = {"xs": ("dram", [4, 128, 1024], "bfloat16")}
-for _n, _w, _d in (("W0", NW, "bfloat16"), ("W1", NW, "bfloat16"), ("W2", NW, "bfloat16"), ("R3", 1024, "bfloat16"),
-                   ("YL", 4096, "bfloat16"), ("RL", 576, "bfloat16"), ("QS", 576, "bfloat16"), ("FW", 384, "bfloat16"),
-                   ("FP", 24, "uint16"), ("LQ", 72, "uint16"), ("PB", 24, "uint16"), ("LM", 256, "uint16"),
-                   ("TAB", 256, "float32"), ("TG", 1024, "float32"), ("GA", 4096, "bfloat16"), ("SC", 4096, "bfloat16"),
-                   ("GQ", 960, "bfloat16"), ("SQ", 960, "bfloat16"), ("MM", 1280, "bfloat16"), ("MQ", 960, "bfloat16"),
-                   ("S8", 1024, "float32"), ("S2", 256, "float32"), ("RB", 512, "bfloat16"), ("IS", 256, "bfloat16"),
-                   ("TRI", 128, "bfloat16"), ("DM", 128, "bfloat16"), ("SH", 128, "bfloat16"), ("TB", 4, "bfloat16"),
-                   ("RT", 640, "bfloat16"), ("DS", 644, "bfloat16"), ("CP", 768, "bfloat16"), ("SEG", 384, "float32"),
-                   ("FF", 512, "float32"), ("CC", 384, "float32"), ("EE", 768, "float32"), ("EV", 768, "float32"),
-                   ("JK", 768, "float32"), ("TT", 384, "float32"), ("UU", 384, "float32"), ("REP", 128, "float32"),
-                   ("ROW", 128, "float32"), ("NBI", 128, "int32"), ("VI", 128, "int32")):
+VN, DC = 64, 192
+CUTS = ([0, VN, DC, 352, 512], [0, VN, DC, 352, 512], [0, VN, 256, 384, 512])
+YC = (0, 256, 512)
+SCRATCH = {"xs": ("dram", [8, 128, 512], "bfloat16"), "Y0": ("dram", [8, 128, YC[1]], "bfloat16"),
+           "Y1": ("dram", [8, 128, YC[2] - YC[1]], "bfloat16")}
+for _n, _w, _d in (("W0", NW, "bfloat16"), ("W1", NW, "bfloat16"), ("W2", NW, "bfloat16"), ("R3", 512, "bfloat16"),
+                   ("RL", 288, "bfloat16"), ("QS", 288, "bfloat16"),
+                   ("FP", 12, "uint16"), ("LQ", 36, "uint16"), ("PB", 12, "uint16"), ("LM", 128, "uint16"), ("TU", 128, "uint16"),
+                   ("TH", 256, "bfloat16"), ("TG", 1024, "float32"),
+                   ("GA", 2048, "bfloat16"), ("SC", 2048, "bfloat16"), ("GQ", 480, "bfloat16"), ("SQ", 480, "bfloat16"),
+                   ("MM", 1024, "bfloat16"), ("MQ", 480, "bfloat16"), ("S8", 1024, "bfloat16"), ("S2", 128, "float32"),
+                   ("RB", 1024, "bfloat16"), ("SF", 256, "bfloat16"), ("BD", 512, "float32"), ("LL", 256, "float32"),
+                   ("DG", 384, "float32"), ("DI", 384, "float32"), ("RM", 384, "float32"), ("DD", 384, "float32"),
+                   ("DE", 384, "float32"), ("TRI", 128, "bfloat16"), ("DM", 128, "bfloat16"), ("SH", 128, "bfloat16"),
+                   ("TB", 4, "bfloat16"), ("RT", 640, "bfloat16"), ("DS", 644, "bfloat16"), ("CP", 768, "bfloat16"),
+                   ("SEG", 384, "float32"), ("FF", 512, "float32"), ("CC", 384, "float32"), ("EE", 768, "float32"),
+                   ("EV", 768, "float32"), ("JK", 768, "float32"), ("TT", 384, "float32"), ("UU", 384, "float32"),
+                   ("IS", 256, "float32"), ("IB", 640, "bfloat16"), ("NU", 128, "uint16"), ("NBI", 128, "int32"),
+                   ("VI", 128, "int32")):
     SCRATCH[_n] = ("sbuf", [128, _w], _d)
 for _k in range(8):
     SCRATCH["P%d" % _k] = ("psum", [128, 512], "float32")
 PACK = {}
-for _b, _d, _l in (("PU", "uint16", "OFP 12 CU 12 AU 12 CL 48"),
-                   ("PN", "int32", "CI 12 C2 12 A2 12 PI 1 PC 8 OWN 128 LO 128 HI 128 VQ 12 OI 12 OJ 12 VR 128 VS 128"),
-                   ("PX", "float32", "NB 192 NM 192 R2A 192 R2B 192 CA 48 CM 48 CY 48 CZ 48 CO 48 PF 8 R16 16 KC 1 KC2 1 RC 1 "
-                    "H1 1 H2 1 H3 1 HM 16 M8 8 M4 4 SCOL 2 VC 6 RW 48 BC 3 R1 128 R4 128 LV 128 LR 128")):
+for _b, _d, _l in (("PU", "uint16", "OFP 6 CU 6 AU 6 CL 24"),
+                   ("PN", "int32", "CI 6 C2 6 A2 6 PI 1 PC 8 OWN 128 LO 128 HI 128 OI 6 OJ 6 TI 128 VR 128 VS 128 "
+                    "GI 128 SA 128 SB 128 TJ 128 TK 128"),
+                   ("PX", "float32", "NB 96 NM 96 CA 24 CM 24 CY 24 CZ 24 CO 24 PF 8 KM 8 KC 1 KC2 1 RC 1 SC2 1 "
+                    "M2 2 M4 4 MJ 4 SCOL 2 VC 6 RW 12 BC 3 R1 128 R4 128 R5 128 R6 128 R7 128 TAB 128 TAR 128 LV 128 LT 128 "
+                    "LD 128 LE 128")):
     _l, _o = _l.split(), 0
     for _k in range(0, len(_l), 2):
         PACK[_l[_k]] = (_b, _o, int(_l[_k + 1]))
         _o += (int(_l[_k + 1]) + 7) // 8 * 8
     SCRATCH[_b] = ("sbuf", [128, _o], _d)
-SEMAPHORES = ("v s p gi ls dn dx do dw0 dw1 dw2 dy ax at aq ar0 ar1 ar2 rq rr0 rr1 rr2".split()
-              + ["ay%d%d" % (q, c) for q in range(4) for c in range(2)])
+SEMAPHORES = ("v s p gi ls lx dn dx dz do dw0 dw1 dw2 dy ax at an aq rq ar0 ar1 ar2".split()
+              + ["ay%d%d" % (m, c) for m in range(8) for c in range(2)])
 BIG = 9.99e29
 
 
@@ -39,14 +48,17 @@ def bits(m):
 def places(T, topo):
     near = lambda a, b: topo.host(a) == topo.host(b) and topo.chip(a) == topo.chip(b)
     world = range(512)
-    teams = [[c for c in world if near(c, k) and topo.die(c) == topo.die(k)] for k in T.cores]
-    relay = {}
-    for t in teams:
-        for s in t:
-            here = [c for c in world if near(c, s)]
-            there = [c for c in world if topo.same_plane(s, c) and topo.chip(c) == topo.chip(s)]
-            relay[s] = there[here.index(s)]
-    return teams, relay
+    teams = []
+    for k in T.cores:
+        on = [c for c in world if near(c, k) and topo.die(c) == topo.die(k)]
+        here = [c for c in world if near(c, k)]
+        there = [c for c in world if topo.same_plane(k, c) and topo.chip(c) == topo.chip(k)]
+        off = [there[here.index(c)] for c in on]
+        team = on + off
+        if teams and not topo.may_write(teams[0][0], team[0]):
+            team = off + on
+        teams.append(team)
+    return teams
 
 
 def others(r):
@@ -59,13 +71,10 @@ _cache = {}
 def rank_program(g, core, T, topo):
     if "p" not in _cache:
         _cache["p"] = places(T, topo)
-    teams, relay = _cache["p"]
+    teams = _cache["p"]
     for r in range(4):
         if core in teams[r]:
-            return team_program(g, core, T, topo, teams, relay, r, teams[r].index(core))
-    for s in relay:
-        if relay[s] == core:
-            return relay_program(g, core, T, topo, teams, s)
+            return team_program(g, core, T, topo, teams, r, teams[r].index(core))
 
 
 def dst(topo, d, core):
@@ -73,44 +82,17 @@ def dst(topo, d, core):
     return DstId(rid=rid, pnc=pid)
 
 
-def cross(teams, topo, r):
-    return [o for o in others(r) if topo.host(teams[o][0]) != topo.host(teams[r][0])]
-
-
-def relay_program(g, core, T, topo, teams, s):
-    r = [k for k in range(4) if s in teams[k]][0]
-    q, far, n = teams[r].index(s), cross(teams, topo, r), 0
-    e = bits(topo.mask(core, teams[far[0]][q]))
-    if s == T.cores[r]:
-        g.wait_ge(T.sem["rq"], 8)
-        tr = []
-        for h, o in enumerate(far):
-            ri = others(o).index(r)
-            tr.append(RemoteDMATransfer(dst_ids=[dst(topo, d, core) for d in teams[o]], srcs=[T.FP[:]],
-                                        dsts=[T.LQ[:, 24 * ri:24 * ri + 24] for d in teams[o]],
-                                        dma_engine_mask=sum(e[4 * h:4 * h + 4]), remote_sem=T.sem["aq"]))
-        g.remote_dma_fused(tr, local_sem=T.sem["ls"])
-        n += 8
-    for k in range(3):
-        g.wait_ge(T.sem["rr%d" % k], 8)
-        tr = []
-        for h, o in enumerate(far):
-            c, f = 192 * k + 64 * others(o).index(r), 128 * k + 64 * h
-            tr.append(RemoteDMATransfer(dst_ids=[dst(topo, teams[o][q], core)], srcs=[T.FW[:, f:f + 64]],
-                                        dsts=[T.RL[:, c:c + 64]],
-                                        dma_engine_mask=sum(e[4 * h:4 * h + 4]), remote_sem=T.sem["ar%d" % k]))
-        g.remote_dma_fused(tr, local_sem=T.sem["ls"])
-        n += 8
-    g.wait_ge(T.sem["ls"], n)
-
-
-def team_program(g, core, T, topo, teams, relay, r, q):
-    home = T.cores[r]
+def team_program(g, core, T, topo, teams, r, m):
+    home, team = T.cores[r], teams[r]
     isr = core == home
-    oth, far = others(r), cross(teams, topo, r)
-    mate = [o for o in oth if o not in far][0]
-    en_on, en_off = bits(topo.mask(core, teams[mate][q])), bits(topo.mask(core, relay[core]))
+    oth = others(r)
+    near = lambda a, b: topo.host(a) == topo.host(b) and topo.chip(a) == topo.chip(b)
+    mate = [o for o in oth if near(teams[o][m], core)][0]
+    far = [o for o in oth if o != mate]
+    en_on, en_off = bits(topo.mask(core, teams[mate][m])), bits(topo.mask(core, teams[far[0]][m]))
     en_hi = [b for b in en_on if b not in en_off]
+    own_chip = [c for c in team if c != core and near(c, core)]
+    off_chip = [c for c in team if not near(c, core)]
     A, S = AluOpType, T.sem
     COPY = ActivationFunctionType.Copy
     queue = {"v": g.vector, "s": g.scalar, "p": g.tensor, "g": g, "y": g.sync}
@@ -149,95 +131,107 @@ def team_program(g, core, T, topo, teams, relay, r, q):
     def mm(out, l, rh, st=True, sp=True):
         return inc(g.tensor.matmul(out, l, rh, st, sp), "p", 1)
 
-    def iota(out, pat, cm=0):
-        if cm:
-            return inc(g.iota(out, pat, 0, cm), "gi", 1)
-        return inc(g.iota(out, pat, 0, 0, allow_small_or_imprecise_dtypes=True), "gi", 1)
-
-    def select(buf, pat, base, cm, op, fillv=0.0):
-        return inc(g.affine_select(buf, buf, pat, op, fillv, base, cm), "gi", 1)
+    def iota(out, pat, base=0, cm=0, ints=False):
+        if ints:
+            return inc(g.iota(out, pat, base, cm), "gi", 1)
+        return inc(g.iota(out, pat, base, cm, allow_small_or_imprecise_dtypes=True), "gi", 1)
 
     def rotate(W, c0, c1, sem):
-        for k in (1, 2, 3):
-            a = 32 * k
-            inc(g.sync.dma_start(W[0:128 - a, 1024 * k + c0:1024 * k + c1], W[a:128, c0:c1]), sem, 16)
-            inc(g.sync.dma_start(W[128 - a:128, 1024 * k + c0:1024 * k + c1], W[0:a, c0:c1]), sem, 16)
+        for k in range(1, 8):
+            a = 16 * k
+            inc(g.sync.dma_start(W[0:128 - a, 512 * k + c0:512 * k + c1], W[a:128, c0:c1]), sem, 16)
+            inc(g.sync.dma_start(W[128 - a:128, 512 * k + c0:512 * k + c1], W[0:a, c0:c1]), sem, 16)
+
+    def fused(parts, left="ls"):
+        tr = [RemoteDMATransfer(dst_ids=[dst(topo, d, core) for d in ds], srcs=[src], dsts=to, dma_engine_mask=sum(e),
+                                remote_sem=S[sem]) for ds, src, to, e, sem in parts]
+        g.remote_dma_fused(tr, local_sem=S[left])
+        n[left] = n.get(left, 0) + sum(len(p[3]) for p in parts)
+
+    def to_team(src, to, sem):
+        fused([(off_chip, src, [to for c in off_chip], en_off, sem), (own_chip, src, [to for c in own_chip], en_hi, sem)])
 
     W = [T.W0, T.W1, T.W2, T.R3]
     PS = [T["P%d" % k] for k in range(8)]
     if isr:
         inc(g.sync.dma_start(T.NBI[:], T.nb[:]), "dn", 16)
-        for b in range(4):
-            inc(g.sync.dma_start(T.xs[:, 32 * b:32 * b + 32, :], T.x[:, 1024 * b:1024 * b + 1024]), "dx", 16)
-        for b in range(4):
-            inc(g.scalar.dma_start(T.W0[32 * b:32 * b + 32, 0:1024], T.x[32 * q:32 * q + 32, 1024 * b:1024 * b + 1024]),
-                "do", 16)
-    iota(u("PI"), [[0, 1]], 1)
-    iota(u("R16"), [[1, 16]])
-    iota(T.ROW[:], [[0, 8], [1, 16]])
-    if isr:
-        iota(T.IS[:], [[1, 256]])
-        for b in (T.TRI[:], T.SH[:], T.DM[:]):
-            v0 = V(fill, b, 1.0, free=True)
-        V(fill, T.SEG[:], 1.0)
-        V(fill, T.SEG[:, 0:384:128], 0.0)
-    gc1 = n["gi"]
-    for b in (T.S8[:], T.S2[:], T.RB[:]):
-        vf = V(fill, b, 1.0, free=True)
+        zf = team.index(off_chip[0])
+        for z, sem in ((zf, "dx"), (4 - zf, "dz")):
+            for b in range(8):
+                inc(g.sync.dma_start(T.xs[z:z + 4, 16 * b:16 * b + 16, :], T.x[16 * z:16 * z + 64, 512 * b:512 * b + 512]), sem, 16)
+        for b in range(8):
+            inc(g.scalar.dma_start(T.W0[16 * b:16 * b + 16, 0:512], T.x[16 * m:16 * m + 16, 512 * b:512 * b + 512]), "do", 16)
+    IR, ROWM, ROW8, ROWG = [T.IB[:, a:a + 128] for a in (0, 256, 384, 512)]
+    iota(u("PI"), [[0, 1]], 0, 1, True)
+    gc0 = iota(T.IB[:, 0:256], [[0, 2], [1, 128]])
+    iota(T.IS[:], [[1, 256]])
+    iota(ROWM, [[0, 8], [1, 16]])
+    iota(ROW8, [[1, 8], [8, 16]])
+    gc1 = iota(ROWG, [[1, 8], [0, 16]])
+    gc2 = n["gi"]
+    if not isr:
+        gc2 = iota(T.DG[:], [[0, 24], [1, 16]])
     pf = lambda c: u("PF", c, c + 1)
-
-    def small_constants():
-        for c, (sh, am) in enumerate([(5, 3), (4, 7), (0, 15), (2, 3), (4, 1), (0, 3), (0, 127), (1, 3)]):
-            V(ts, u("PC", c, c + 1), u("PI"), sh, am, A.logical_shift_right, A.bitwise_and, free=c > 0)
-        V(cp, u("PF"), u("PC"))
-        V(ts, u("SCOL", 0, 1), pf(6), 1.0, None, A.add)
-        V(ts, u("SCOL", 1, 2), pf(6), 129.0, None, A.add, free=True)
-        V(ts, u("KC"), pf(0), 1024.0, None, A.mult, free=True)
-        V(ts, u("KC2"), pf(0), -1024.0, 4096.0, A.mult, A.add, free=True)
-        V(ts, u("RC"), pf(7), -1024.0, 4096.0, A.mult, A.add, free=True)
-        V(ts, u("H1"), pf(0), 4.0, pf(5), A.mult, A.add, free=True)
-        V(ts, u("H2"), pf(4), -100.0, None, A.mult, free=True)
-        V(ts, u("M8"), u("R16", 0, 8), pf(1), None, A.is_equal, free=True)
-        V(ts, u("M4"), u("R16", 0, 4), pf(3), None, A.is_equal, free=True)
-        V(ts, T.REP[:], T.ROW[:], pf(2), None, A.is_equal, free=True)
-        V(tt, u("H3"), u("H1"), u("H2"), A.add)
-        V(ts, u("HM"), u("R16"), u("H3"), None, A.is_equal)
-
-    def late_fills():
-        for b, c in ((T.MM[:], BIG), (T.MQ[:], BIG), (u("R2A"), 0.0), (u("R2B"), 0.0)):
-            V(fill, b, c, free=True)
-        V(fill, T.MM[:, 0:1280:4], -BIG)
-        V(fill, T.MQ[:, 0:960:5], -BIG, free=True)
-
-    def selectors():
-        wait("g", "v", vf)
-        select(T.S2[:, 0:128], [[-2, 4], [0, 2], [-8, 16]], 0, 1, A.is_equal)
-        select(T.S2[:, 128:256], [[-2, 4], [0, 2], [-8, 16]], -1, 1, A.is_equal)
-        select(T.S8[:], [[-1, 8], [0, 8], [-8, 16]], 0, 1, A.is_equal)
-        select(T.RB[:], [[-32, 4], [0, 4], [-1, 32]], 0, 1, A.is_equal)
-
-    wait("v", "gi", gc1)
+    wait("v", "gi", gc0)
+    for c, (sh, am) in enumerate([(4, 7), (0, 15), (0, 3), (5, 3), (4, 1), (0, 127), (0, 7), (2, 3)]):
+        V(ts, u("PC", c, c + 1), u("PI"), sh, am, A.logical_shift_right, A.bitwise_and, free=c > 0)
+    V(cp, u("PF"), u("PC"))
+    V(ts, T.TRI[:], IR, pf(5), None, A.is_gt)
+    V(fill, T.SEG[:], 1.0, free=True)
     if isr:
-        wait("g", "gi", gc1)
-        wait("g", "v", v0)
-        select(T.TRI[:], [[1, 128]], 0, -1, A.is_gt)
-        select(T.SH[:], [[1, 128]], -1, -1, A.is_equal)
-        select(T.DM[:], [[1, 128]], 0, -1, A.is_equal)
-        wait("g", "gi")
-        gtri = select(T.DM[:], [[1, 128]], -1, -1, A.not_equal, -1.0)
-        wait("g", "gi")
-        wait("g", "dx")
-        tr = []
-        helpers = [c for c in teams[r] if c != core]
-        for h, c in enumerate(helpers):
-            tr.append(RemoteDMATransfer(dst_ids=[dst(topo, c, core)], srcs=[T.xs[teams[r].index(c)]], dsts=[T.W0[:, 0:1024]],
-                                        dma_engine_mask=sum(en_on[4 * h:4 * h + 4]), remote_sem=S["ax"]))
-        g.remote_dma_fused(tr, local_sem=S["ls"])
-        n["ls"] = n.get("ls", 0) + 12
-        selectors()
-        wait("y", "do")
-        rotate(T.W0, 0, 1024, "dw0")
-        wait("v", "dn")
+        V(ts, T.SH[:], IR, -1.0, pf(5), A.add, A.is_equal, free=True)
+        V(ts, T.CP[:, 0:128], IR, pf(5), None, A.is_equal, free=True)
+        V(tt, T.DM[:], T.CP[:, 0:128], T.SH[:], A.subtract)
+    V(fill, T.SEG[:, 0:384:128], 0.0)
+
+    def request_constants():
+        V(ts, u("SCOL", 0, 1), pf(5), 1.0, None, A.add, free=True)
+        V(ts, u("SCOL", 1, 2), pf(5), 129.0, None, A.add, free=True)
+        V(ts, u("SC2"), pf(3), 16.0, pf(1), A.mult, A.add, free=True)
+        V(ts, u("M2"), T.IB[:, 0:2], pf(4), None, A.is_equal, free=True)
+        V(ts, u("KC2"), pf(0), -512.0, 4096.0, A.mult, A.add, free=True)
+        wait("v", "gi", gc1)
+        V(ts, T.LL[:, 0:128], IR, u("SC2"), None, A.is_equal)
+        V(ts, T.LL[:, 128:256], IR, -64.0, u("SC2"), A.add, A.is_equal, free=True)
+
+    def list_constants():
+        wait("v", "gi", gc1)
+        V(ts, u("RC"), pf(6), -512.0, 4096.0, A.mult, A.add, free=True)
+        V(ts, u("KC"), pf(0), 512.0, None, A.mult, free=True)
+        V(ts, u("KM"), T.IB[:, 0:8], -1.0, pf(5), A.mult, A.add, free=True)
+        V(ts, u("M4"), T.IB[:, 0:4], pf(7), None, A.is_equal, free=True)
+        V(ts, u("MJ"), T.IB[:, 0:4], pf(2), None, A.is_equal, free=True)
+        V(ts, T.S2[:], ROW8, pf(5), None, A.is_equal, free=True)
+        wait("v", "v")
+        for k in range(8):
+            V(ts, T.S8[:, 128 * k:128 * k + 128], ROWM, 8.0, u("KM", k, k + 1), A.mult, A.is_equal, free=True)
+
+    def sweep_constants():
+        wait("v", "gi", gc2)
+        V(ts, T.DI[:], T.DG[:], pf(1), None, A.is_equal, free=True)
+        V(fill, T.RM[:], 1.0, free=True)
+        for j in range(4):
+            V(ts, T.BD[:, 128 * j:128 * j + 128], ROWG, pf(0), u("MJ", j, j + 1), A.is_equal, A.mult, free=j > 0)
+        V(fill, T.RM[:, 0:384:16], 0.0)
+        for b in range(8):
+            V(ts, T.RB[:, 128 * b:128 * b + 128], ROWM, 16.0 * b, pf(5), A.add, A.is_equal, free=True)
+        for b, c in ((T.MM[:], BIG), (T.MQ[:], BIG)):
+            V(fill, b, c, free=True)
+        V(ts, T.SF[:], T.IB[:, 0:256], pf(5), None, A.is_equal, free=True)
+        V(fill, T.MM[:, 0:1024:4], -BIG)
+        V(fill, T.MQ[:, 0:480:5], -BIG, free=True)
+
+    def by_team(src, to, sem):
+        ps = []
+        for h, o in enumerate([mate] + far):
+            e = en_hi[0:4] if o == mate else en_off[4 * (h - 1):4 * h]
+            ps.append(([teams[o][m]], src(o), [to(o)], e, sem))
+        fused(ps)
+
+    def forward(src):
+        by_team(lambda o: src, lambda o: T.LQ[:, 12 * others(o).index(r):12 * others(o).index(r) + 12], "aq")
+
+    def number():
         V(ts, u("OWN"), T.NBI[:], 12, None, A.logical_shift_right)
         V(ts, T.VI[:], T.NBI[:], 4095, None, A.bitwise_and, free=True)
         for i, o in enumerate(oth + [r]):
@@ -245,9 +239,43 @@ def team_program(g, core, T, topo, teams, relay, r, q):
         V(scan, T.CC[:], T.SEG[:], T.FF[:, 0:384], 0.0, A.mult, A.add)
         vt = V(cp, T.TB[:, 0:3], T.CC[:, 127:384:128])
         wait("p", "v", vt)
-        wait("p", "gi", gtri)
         pbase = mm(PS[3][:, 0:3], T.TRI[:], T.TB[:, 0:3])
         V(tt, T.RT[:, 0:384], T.CC[:], T.FF[:, 0:384], A.mult)
+        return pbase
+
+    def codes():
+        for i in range(3):
+            V(ts, u("BC", i, i + 1), PS[3][:, i:i + 1], 4095.0 + 256 * i, None, A.add, free=i > 0)
+        for i in range(3):
+            c = slice(128 * i, 128 * i + 128)
+            V(ts, T.TT[:, c], T.FF[:, c], u("BC", i, i + 1), None, A.mult, free=i > 0)
+        V(tt, u("LV"), T.FF[:, 384:512], T.VI[:], A.mult, free=True)
+        V(tt, T.UU[:], T.TT[:], T.RT[:, 0:384], A.add)
+        V(tt, u("R1"), T.UU[:, 0:128], T.UU[:, 128:256], A.add)
+        V(tt, u("R4"), u("R1"), T.UU[:, 256:384], A.add)
+        V(cp, u("GI"), u("R4"))
+        V(tt, u("R5"), u("R4"), u("LV"), A.add, free=True)
+        V(ts, u("SA"), u("GI"), 224, None, A.bitwise_and)
+        V(ts, u("SB"), u("GI"), 768, None, A.bitwise_and, free=True)
+        V(ts, u("R6"), u("SA"), 2.0, None, A.mult)
+        V(ts, u("R7"), u("SB"), -0.875, None, A.mult, free=True)
+        V(tt, u("R1"), u("R5"), u("R6"), A.add)
+        V(tt, u("R6"), u("R1"), u("R7"), A.add)
+        return V(cp, T.TU[:], u("R6"))
+
+    if isr:
+        wait("v", "dn")
+        vnu = V(cp, T.NU[:], T.NBI[:])
+        wait("g", "v", vnu)
+        to_team(T.NU[:], T.NU[:], "an")
+        wait("g", "dx")
+        fused([([c], T.xs[team.index(c)], [T.W0[:, 0:512]], en_off[2 * h:2 * h + 2], "ax") for h, c in enumerate(off_chip)], "lx")
+        wait("g", "dz")
+        fused([([c], T.xs[team.index(c)], [T.W0[:, 0:512]], en_hi[2 * h:2 * h + 2], "ax") for h, c in enumerate(own_chip)], "lx")
+        wait("y", "do")
+        wait("y", "lx")
+        rotate(T.W0, 0, 512, "dw0")
+        pbase = number()
         V(ts, u("HI"), T.VI[:], 4032, None, A.bitwise_and, free=True)
         V(ts, u("LO"), T.VI[:], 63, None, A.bitwise_and, free=True)
         V(cp, T.RT[:, 384:512], u("HI"))
@@ -261,9 +289,10 @@ def team_program(g, core, T, topo, teams, relay, r, q):
         act(T.DS[:, 0:384], PS[4][:, 0:384])
         sd = act(T.DS[:, 384:643], PS[5][:, 0:259], free=True)
         wait("v", "p", pbase)
+        wait("v", "gi", gc1)
         for i in range(3):
             vcp = V(ts, T.CP[:, 256 * i:256 * i + 256], T.IS[:], PS[3][:, i:i + 1], None, A.is_ge, free=i > 0)
-        small_constants()
+        request_constants()
         wait("p", "v", vcp)
         wait("p", "s", sd)
         vev, ptl = {}, {}
@@ -288,105 +317,95 @@ def team_program(g, core, T, topo, teams, relay, r, q):
             if t + 3 < 6:
                 tile(t + 3)
             wait("s", "v", vev[t])
-            sacc = act(T.JK[:, c], T.EV[:, c], u("VC", t, t + 1))
+            sacc = act(T.JK[:, c], T.EV[:, c], u("VC", t, t + 1), free=True)
         wait("v", "s", sacc)
         for t in range(6):
-            i, h = t // 2, t % 2
-            for kk in range(2):
-                a = 12 * (2 * h + kk) + 4 * i
-                vw = V(ts, u("RW", a, a + 4), u("M8", 4 * kk, 4 * kk + 4), u("VC", t, t + 1), None, A.mult, free=t + kk > 0)
+            a = 6 * (t % 2) + 2 * (t // 2)
+            vw = V(ts, u("RW", a, a + 2), u("M2"), u("VC", t, t + 1), None, A.mult, free=t > 0)
         wait("p", "v", vw)
-        wait("p", "p")
-        pw = mm(PS[6][:, 0:48], T.REP[:], u("RW"))
+        mm(PS[6][:, 0:6], T.LL[:, 0:128], u("RW", 0, 6), True, False)
+        pw = mm(PS[6][:, 0:6], T.LL[:, 128:256], u("RW", 6, 12), False, True)
         wait("v", "p", pw)
-        for k in range(4):
-            p = slice(32 * k, 32 * k + 32)
-            V(cp, u("VQ", p=p), PS[6][p, 12 * k:12 * k + 12], free=k > 0)
-        V(ts, u("OI"), u("VQ"), u("KC2"), None, A.add)
+        V(ts, u("OI"), PS[6][:, 0:6], u("KC2"), None, A.add)
+        V(cp, T.PB[:, 6:12], PS[6][:, 0:6], free=True)
         V(ts, u("OJ"), u("OI"), 4095, None, A.bitwise_and)
-        V(cp, T.PB[:, 0:12], u("OJ"))
-        vpb = V(cp, T.PB[:, 12:24], u("VQ"), free=True)
+        vpb = V(cp, T.PB[:, 0:6], u("OJ"))
         wait("g", "v", vpb)
-        ri = others(mate).index(r)
-        g.remote_dma_fused([
-            RemoteDMATransfer(dst_ids=[dst(topo, relay[core], core)], srcs=[T.PB[:]], dsts=[T.FP[:]],
-                              dma_engine_mask=sum(en_off), remote_sem=S["rq"]),
-            RemoteDMATransfer(dst_ids=[dst(topo, d, core) for d in teams[mate]], srcs=[T.PB[:]],
-                              dsts=[T.LQ[:, 24 * ri:24 * ri + 24] for d in teams[mate]],
-                              dma_engine_mask=sum(en_hi), remote_sem=S["aq"])], local_sem=S["ls"])
-        n["ls"] += 16
-        for i in range(3):
-            V(ts, u("BC", i, i + 1), PS[3][:, i:i + 1], 4095.0 + 256 * i, None, A.add, free=i > 0)
-        for i in range(3):
-            c = slice(128 * i, 128 * i + 128)
-            V(ts, T.TT[:, c], T.FF[:, c], u("BC", i, i + 1), None, A.mult, free=i > 0)
-        V(ts, u("VS"), T.VI[:], u("RC"), None, A.add, free=True)
-        V(tt, u("LV"), T.FF[:, 384:512], T.VI[:], A.mult, free=True)
-        V(tt, T.UU[:], T.TT[:], T.RT[:, 0:384], A.add)
-        V(ts, u("VR"), u("VS"), 4095, None, A.bitwise_and, free=True)
-        V(tt, u("R1"), T.UU[:, 0:128], T.UU[:, 128:256], A.add)
-        V(tt, u("LR"), T.FF[:, 384:512], u("VR"), A.mult, free=True)
-        V(tt, u("R4"), u("R1"), T.UU[:, 256:384], A.add)
-        V(tt, T.TAB[:, 0:128], u("R4"), u("LV"), A.add)
-        vtab = V(tt, T.TAB[:, 128:256], u("R4"), u("LR"), A.add, free=True)
-        wait("g", "v", vtab)
-        g.remote_dma_fused([
-            RemoteDMATransfer(dst_ids=[dst(topo, c, core) for c in helpers], srcs=[T.TAB[:]], dsts=[T.TAB[:] for c in helpers],
-                              dma_engine_mask=sum(en_on), remote_sem=S["at"])], local_sem=S["ls"])
-        n["ls"] += 16
-        wait("p", "v", vtab)
-        wait("v", "v")
+        to_team(T.PB[:], T.FP[:], "rq")
+        forward(T.PB[:])
+        gc2 = iota(T.DG[:], [[0, 24], [1, 16]])
+        n["aq"], n["at"] = 12, len(en_on)
+        list_constants()
+        sweep_constants()
+        wait("v", "at")
     else:
-        wait("v", "v")
-        small_constants()
-        selectors()
-        n["ax"], n["at"] = 4, 16
+        n["ax"], n["rq"], n["aq"], n["an"] = 2, 8, 12, 8
         wait("y", "ax")
-        rotate(T.W0, 0, 1024, "dw0")
-        wait("p", "v")
+        rotate(T.W0, 0, 512, "dw0")
+        list_constants()
+        sweep_constants()
+        wait("v", "an")
+        V(cp, T.NBI[:], T.NU[:])
         wait("v", "v")
-        wait("p", "at")
-    late_fills()
-    wait("p", "gi")
+        pbase = number()
+        wait("v", "p", pbase)
+        vtu = codes()
+        if core == [c for c in team if c != home and near(c, home)][0]:
+            wait("g", "v", vtu)
+            rid, pid = topo.addr(home, core)
+            g.remote_dma(T.TU[:], T.TU[:], S["at"], S["ls"], pid, rid, topo.mask(core, home))
+            n["ls"] = n.get("ls", 0) + len(en_on)
+        wait("g", "rq")
+        forward(T.FP[:])
+    V(cp, u("TI"), T.TU[:])
+    V(cp, u("TAB"), T.TU[:], free=True)
+    V(ts, u("VS"), u("TI"), u("RC"), None, A.add)
+    V(ts, u("LT"), u("TAB"), 4096.0, None, A.is_lt, free=True)
+    V(ts, u("VR"), u("VS"), 4095, None, A.bitwise_and)
+    V(ts, u("TJ"), u("TI"), 8128, None, A.bitwise_and, free=True)
+    V(tt, u("LD"), u("VR"), u("TAB"), A.subtract)
+    V(ts, u("TK"), u("TI"), 63, None, A.bitwise_and, free=True)
+    V(tt, u("LE"), u("LD"), u("LT"), A.mult)
+    vtr = V(tt, u("TAR"), u("LE"), u("TAB"), A.add)
+    wait("p", "v", vtr)
     wait("p", "s")
     wait("p", "p")
-    mm(PS[6][:, 0:128], T.S2[:, 0:128], T.TAB[:, 128:256])
-    mm(PS[6][:, 128:256], T.S2[:, 128:256], T.TAB[:, 128:256])
-    for m in range(8):
-        pg = mm(PS[4 + m // 4][:, 128 * (m % 4):128 * (m % 4) + 128], T.S8[:, 128 * m:128 * m + 128], T.TAB[:, 0:128])
-    n["aq"] = 16
-    cols = [24 * ri + 4 * others(o).index(r) for ri, o in enumerate(oth)]
+    pl = mm(PS[6][:, 0:128], T.S2[:], u("TAR"))
+    V(cp, T.TH[:, 0:128], u("TJ"), free=True)
+    vth = V(cp, T.TH[:, 128:256], u("TK"), free=True)
+    wait("p", "v", vth)
+    ptg = []
+    for k in range(8):
+        o = PS[4 + k // 4][:, 128 * (k % 4):128 * (k % 4) + 128]
+        mm(o, T.S8[:, 128 * k:128 * k + 128], T.TH[:, 0:128], True, False)
+        ptg.append(mm(o, T.S8[:, 128 * k:128 * k + 128], T.TH[:, 128:256], False, True))
+    cols = [12 * ri + 2 * others(o).index(r) for ri, o in enumerate(oth)]
     src = "do" if isr else "ax"
     wait("s", "aq")
     wait("s", "dw0")
     wait("s", src)
     for ri in range(3):
-        sq = act(T.QS[:, 64 * ri:64 * ri + 64], T.W0[:, 0:4096].indirect(T.LQ[:, cols[ri]:cols[ri] + 4]), free=True)
+        sq = act(T.QS[:, 32 * ri:32 * ri + 32], T.W0[:, 0:4096].indirect(T.LQ[:, cols[ri]:cols[ri] + 2]), free=True)
 
     def send(k, sem, val):
         wait("g", sem, val)
-        tr = []
-        for h, o in enumerate(far):
-            a, f = 192 * k + 64 * oth.index(o), 128 * k + 64 * h
-            tr.append(RemoteDMATransfer(dst_ids=[dst(topo, relay[core], core)], srcs=[T.QS[:, a:a + 64]],
-                                        dsts=[T.FW[:, f:f + 64]],
-                                        dma_engine_mask=sum(en_off[4 * h:4 * h + 4]), remote_sem=S["rr%d" % k]))
-        a, c = 192 * k + 64 * oth.index(mate), 192 * k + 64 * others(mate).index(r)
-        tr.append(RemoteDMATransfer(dst_ids=[dst(topo, teams[mate][q], core)], srcs=[T.QS[:, a:a + 64]],
-                                    dsts=[T.RL[:, c:c + 64]],
-                                    dma_engine_mask=sum(en_hi[0:4]), remote_sem=S["ar%d" % k]))
-        g.remote_dma_fused(tr, local_sem=S["ls"])
-        n["ls"] = n.get("ls", 0) + 12
+
+        def at(o):
+            c = 96 * k + 32 * others(o).index(r)
+            return T.RL[:, c:c + 32]
+        by_team(lambda o: T.QS[:, 96 * k + 32 * oth.index(o):96 * k + 32 * oth.index(o) + 32], at, "ar%d" % k)
 
     send(0, "s", sq)
-    wait("v", "p", pg)
-    V(cp, T.LM[:], PS[6][:, 0:256])
+    wait("v", "p", pl)
+    vlm = V(cp, T.LM[:], PS[6][:, 0:128])
+    wait("v", "p", ptg[3])
     V(cp, T.TG[:, 0:512], PS[4][:], free=True)
+    wait("v", "p", ptg[7])
     V(cp, T.TG[:, 512:1024], PS[5][:], free=True)
     wait("v", "aq")
     for ri in range(3):
-        V(cp, u("CI", 4 * ri, 4 * ri + 4), T.LQ[:, cols[ri] + 12:cols[ri] + 16], free=True)
-        V(cp, u("OFP", 4 * ri, 4 * ri + 4), T.LQ[:, cols[ri]:cols[ri] + 4], free=True)
+        V(cp, u("CI", 2 * ri, 2 * ri + 2), T.LQ[:, cols[ri] + 6:cols[ri] + 8], free=True)
+        V(cp, u("OFP", 2 * ri, 2 * ri + 2), T.LQ[:, cols[ri]:cols[ri] + 2], free=True)
     V(ts, u("C2"), u("CI"), 2, None, A.logical_shift_right)
     V(ts, u("A2"), u("CI"), 3, None, A.bitwise_and, free=True)
     V(cp, u("CU"), u("C2"))
@@ -395,95 +414,124 @@ def team_program(g, core, T, topo, teams, relay, r, q):
     vnm = V(tt, u("NM"), u("M4").indirect(u("AU")), u("NB"), A.mult)
     wait("p", "v", vnm)
     wait("p", "p")
-    lo96 = slice(0, 96)
-    mm(PS[7][lo96, 0:16], u("NM", 0, 96), u("HM"))
-    po = mm(PS[7][lo96, 16:32], u("NM", 96, 192), u("HM"))
+    for j in range(4):
+        po = mm(PS[7][:, 96 * j:96 * j + 96], T.BD[:, 128 * j:128 * j + 128], u("NM"))
     wait("v", "p", po)
-    for t, R2 in enumerate(("R2A", "R2B")):
-        for c in range(6):
-            vr2 = V(ts, u(R2, 6 * t + c, 192, lo96, 12), PS[7][lo96, 16 * t:16 * t + 16], u("M8", c, c + 1, lo96), None, A.mult,
-                    free=t + c > 0)
-    wait("p", "v", vr2)
-    wait("p", "p")
-    mm(PS[6][:, 0:192], T.REP[lo96, :], u("R2A", p=lo96), True, False)
-    pc = mm(PS[6][:, 0:192], T.REP[lo96, :], u("R2B", p=lo96), False, True)
-    wait("v", "p", pc)
-    for b in range(4):
-        p = slice(32 * b, 32 * b + 32)
-        V(cp, u("CA", p=p), PS[6][p, 48 * b:48 * b + 48], free=b > 0)
+    vdd = V(tt, T.DD[:], T.DI[:], PS[7][:, 0:384], A.mult)
+    V(scan, T.DE[:], T.RM[:], T.DD[:], 0.0, A.mult, A.add)
+    V(cp, u("CA"), T.DE[:, 15:384:16])
     V(ts, u("CM"), u("CA"), 4096.0, u("KC"), A.is_lt, A.mult)
     V(tt, u("CY"), u("CA"), u("CM"), A.subtract)
     V(ts, u("CZ"), u("CY"), 0.0, 4096.0, A.is_lt, A.mult)
     V(tt, u("CO"), u("CY"), u("CZ"), A.add)
     V(cp, u("CL"), u("CO"))
-    cuts = [0, 192, 512, 768, 928, 1024]
-    for k in range(3):
-        w, nxt = W[k], W[k + 1]
+    own = PS[7]
+
+    def spread(k):
         n["ar%d" % k] = 12
         wait("p", "ar%d" % k)
-        wait("p", "v")
-        wait("p", "p")
-        for i in range(3):
-            for b in range(4):
-                c, a = 256 * i + 64 * b, 192 * k + 64 * i
-                pr = mm(PS[4 + c // 512][:, c % 512:c % 512 + 64], T.RB[:, 128 * b:128 * b + 128], T.RL[:, a:a + 64])
-        wait("s", "p", pr)
-        wait("v", "p", pr)
-        sr = act(w[:, 4096:4608], PS[4][:])
-        vr = V(cp, w[:, 4608:4864], PS[5][:, 0:256])
+        for b in range(8):
+            c = 96 * b if b < 5 else 96 * (b - 5)
+            pr = mm(PS[4 + b // 5][:, c:c + 96], T.RB[:, 128 * b:128 * b + 128], T.RL[:, 96 * k:96 * k + 96])
+        return pr
+
+    for k in range(3):
+        w, nxt, cuts, done = W[k], W[k + 1], CUTS[k], {}
+
+        def main():
+            for c in range(1 if k else 0, len(cuts) - 1):
+                a, b = cuts[c], cuts[c + 1]
+                done[c] = act(T.GA[:, 4 * a:4 * b], w[:, 0:NW].indirect(T.LM[:, a // 4:b // 4]), free=True)
+
+        if k == 0:
+            wait("p", "v", vdd)
+            wait("p", src)
+            wait("p", "s")
+            wait("p", "p")
+            mm(own[:], T.SF[:, 0:128], w[:, 0:512])
+            wait("s", "p", spread(0))
+            act(w[:, 4096:4576], PS[4][:, 0:480])
+            act(w[:, 4576:4864], PS[5][:, 0:288], free=True)
         for e in ("v", "s"):
             wait(e, "dw%d" % k)
             if k == 0:
                 wait(e, src)
-        wait("s", "v", vr)
-        wait("v", "s", sr)
+        wait("s", "v", vlm if k == 0 else None)
+        wait("v", "s")
         wait("s", "s")
         win = w[:, 0:NW]
+        if k == 0:
+            main()
         if k < 2:
-            for j in range(3):
-                V(cp, T.GQ[:, 1 + j:960:5], win.indirect(u("CL", 12 * j, 12 * j + 12)), free=j > 0)
-            act(T.GQ[:, 0:960:5], win.indirect(u("OFP")))
-            sq = act(T.GQ[:, 4:960:5], win.indirect(u("CL", 36, 48)), free=True)
-            wait("v", "s", sq)
+            V(cp, T.GQ[:, 0:480:5], win.indirect(u("OFP")))
+            for j in range(2 if k else 4):
+                V(cp, T.GQ[:, 1 + j:480:5], win.indirect(u("CL", 6 * j, 6 * j + 6)), free=True)
+            if k:
+                for j in range(2, 4):
+                    sq = act(T.GQ[:, 1 + j:480:5], win.indirect(u("CL", 6 * j, 6 * j + 6)), free=True)
+                wait("v", "s", sq)
             V(scan, T.SQ[:], T.MQ[:], T.GQ[:], 0.0, A.min, A.max)
-            vq = V(cp, T.QS[:, 192 * k + 192:192 * k + 384], T.SQ[:, 4:960:5])
+            vq = V(cp, T.QS[:, 96 * k + 96:96 * k + 192], T.SQ[:, 4:480:5])
             send(k + 1, "v", vq)
-        done = {}
-        for c in range(1, 5):
+        if k:
+            main()
+            V(cp, T.GA[:, 0:4 * VN], win.indirect(T.LM[:, 0:VN // 4]))
+        for c in range(len(cuts) - 1):
             a, b = cuts[c], cuts[c + 1]
-            done[c] = act(T.GA[:, 4 * a:4 * b], win.indirect(T.LM[:, a // 4:b // 4]))
-        V(cp, T.GA[:, 0:4 * cuts[1]], win.indirect(T.LM[:, 0:cuts[1] // 4]))
-        for c in range(5):
-            a, b = cuts[c], cuts[c + 1]
-            if c:
+            if c in done:
                 wait("v", "s", done[c])
             V(scan, T.SC[:, 4 * a:4 * b], T.MM[:, 0:4 * (b - a)], T.GA[:, 4 * a:4 * b], 0.0, A.min, A.max)
-            vm = V(tt, nxt[:, a:b], T.SC[:, 4 * a + 3:4 * b:4], w[:, a:b], A.max)
-            if b in (512, 1024):
-                h = b // 512 - 1
-                if k < 2:
-                    wait("y", "v", vm)
-                    rotate(nxt, 512 * h, b, "dw%d" % (k + 1))
-                elif isr:
-                    wait("y", "v", vm)
-                    for bb in range(4):
-                        inc(g.sync.dma_start(T.y[32 * q:32 * q + 32, 1024 * bb + 512 * h:1024 * bb + b],
-                                             nxt[32 * bb:32 * bb + 32, 512 * h:b]), "dy", 16)
+            vm = V(tt, nxt[:, a:b], T.SC[:, 4 * a + 3:4 * b:4], own[:, a:b], A.max)
+            if k < 2 and b == DC:
+                wait("y", "v", vm)
+                rotate(nxt, 0, DC, "dw%d" % (k + 1))
+            elif k < 2 and b == 512:
+                wait("p", "v", vm)
+                e, free = 512 - DC, {}
+                for q in range(1, 8):
+                    bank = (0, 1, 2, 3, 6, 0, 1)[q - 1]
+                    if bank in free:
+                        wait("p", *free[bank])
+                    px = mm(PS[bank][:, 0:e], T.SF[:, 16 * q:16 * q + 128], nxt[:, DC:512])
+                    o = nxt[:, 512 * q + DC:512 * q + 512]
+                    wait("sv"[q % 2], "p", px)
+                    if q % 2:
+                        free[bank] = ("v", V(cp, o, PS[bank][:, 0:e], free=True))
+                    else:
+                        free[bank] = ("s", act(o, PS[bank][:, 0:e], free=True))
+                mm(own[:], T.SF[:, 0:128], nxt[:, 0:512])
+                pr = spread(k + 1)
+                wait("v", "p", pr)
+                wait("s", "p", pr)
+                V(cp, nxt[:, 4096:4576], PS[4][:, 0:480], free=True)
+                act(nxt[:, 4576:4864], PS[5][:, 0:288], free=True)
+            elif k == 2 and b in YC:
+                h = YC.index(b) - 1
+                if isr:
+                    e, eng = (("y", g.sync), ("s", g.scalar))[h]
+                    wait(e, "v", vm)
+                    for bb in range(8):
+                        inc(eng.dma_start(T.y[16 * m:16 * m + 16, 512 * bb + YC[h]:512 * bb + b],
+                                          nxt[16 * bb:16 * bb + 16, YC[h]:b]), "dy", 16)
                 else:
                     wait("g", "v", vm)
                     rid, pid = topo.addr(home, core)
-                    g.remote_dma(T.YL[:, 1024 * q + 512 * h:1024 * q + b], nxt[:, 512 * h:b], S["ay%d%d" % (q, h)], S["ls"],
+                    g.remote_dma(T["Y%d" % h][m], nxt[:, YC[h]:b], S["ay%d%d" % (m, h)], S["ls"],
                                  pid, rid, topo.mask(core, home))
-                    n["ls"] += 16
+                    n["ls"] += len(bits(topo.mask(core, home)))
     if isr:
+        runs = [[i for i in range(8) if near(team[i], core) and i < m], [i for i in range(8) if near(team[i], core) and i > m],
+                [i for i in range(8) if not near(team[i], core)]]
         for h in range(2):
-            for c in helpers:
-                qq = teams[r].index(c)
-                n["ay%d%d" % (qq, h)] = 16
-                for bb in range(4):
+            Y = T["Y%d" % h]
+            for run in [x for x in runs if x]:
+                for i in run:
+                    n["ay%d%d" % (i, h)] = len(bits(topo.mask(team[i], core)))
+                for bb in range(8):
                     e, eng = (("y", g.sync), ("s", g.scalar))[bb % 2]
-                    wait(e, "ay%d%d" % (qq, h))
-                    inc(eng.dma_start(T.y[32 * qq:32 * qq + 32, 1024 * bb + 512 * h:1024 * bb + 512 * h + 512],
-                                      T.YL[32 * bb:32 * bb + 32, 1024 * qq + 512 * h:1024 * qq + 512 * h + 512]), "dy", 16)
+                    for i in run:
+                        wait(e, "ay%d%d" % (i, h))
+                    inc(eng.dma_start(T.y[16 * run[0]:16 * run[-1] + 16, 512 * bb + YC[h]:512 * bb + YC[h + 1]],
+                                      Y[run[0]:run[-1] + 1, 16 * bb:16 * bb + 16, :]), "dy", 16)
     for sem in n:
         wait("g", sem)

@@ -2,41 +2,41 @@ from concourse.bass import DstId, RemoteDMATransfer
 from concourse.mybir import AluOpType, ActivationFunctionType
 
 NW = 4864
-VN, DC = 64, 192
-CUTS = ([0, VN, DC, 352, 512], [0, VN, DC, 352, 512], [0, VN, 256, 384, 512])
+CUTS = ([0, 160, 240, 304, 416, 512], [0, 160, 240, 304, 416, 512], [0, 144, 256, 432, 512])
+PLAN = ("Qs2 Qv0 Qs3 S0 Qv1 E V1 M1 S3 X1 S4 M0 S2 D0 M3 X3 C1 M4 c1 X4 C3 c3 c4 M2 X2 C4 C2 c2",
+        "Qs2 Qv0 Qs3 S0 Qv1 E V1 M1 S3 X1 S4 M0 S2 D0 M3 X3 C1 M4 c1 X4 C3 c3 c4 M2 X2 C4 C2 c2",
+        "V1 S0 S2 M1 M0 Y0 V3 M3 M2 Y1")
 YC = (0, 256, 512)
+BYDMA, BYPE = (1, 2, 3), (4, 5, 6, 7)
 SCRATCH = {"xs": ("dram", [8, 128, 512], "bfloat16"), "Y0": ("dram", [8, 128, YC[1]], "bfloat16"),
            "Y1": ("dram", [8, 128, YC[2] - YC[1]], "bfloat16")}
 for _n, _w, _d in (("W0", NW, "bfloat16"), ("W1", NW, "bfloat16"), ("W2", NW, "bfloat16"), ("R3", 512, "bfloat16"),
                    ("RL", 288, "bfloat16"), ("QS", 288, "bfloat16"),
-                   ("FP", 12, "uint16"), ("LQ", 36, "uint16"), ("PB", 12, "uint16"), ("LM", 128, "uint16"), ("TU", 128, "uint16"),
+                   ("LQ", 36, "uint16"), ("FP", 12, "uint16"), ("PB", 12, "uint16"), ("LM", 128, "uint16"),
                    ("TH", 256, "bfloat16"), ("TG", 1024, "float32"),
                    ("GA", 2048, "bfloat16"), ("SC", 2048, "bfloat16"), ("GQ", 480, "bfloat16"), ("SQ", 480, "bfloat16"),
                    ("MM", 1024, "bfloat16"), ("MQ", 480, "bfloat16"), ("S8", 1024, "bfloat16"), ("S2", 128, "float32"),
-                   ("RB", 1024, "bfloat16"), ("SF", 256, "bfloat16"), ("BD", 512, "float32"), ("LL", 256, "float32"),
+                   ("RB", 1024, "bfloat16"), ("SF", 256, "bfloat16"), ("BD", 512, "float32"),
                    ("DG", 384, "float32"), ("DI", 384, "float32"), ("RM", 384, "float32"), ("DD", 384, "float32"),
-                   ("DE", 384, "float32"), ("TRI", 128, "bfloat16"), ("DM", 128, "bfloat16"), ("SH", 128, "bfloat16"),
-                   ("TB", 4, "bfloat16"), ("RT", 640, "bfloat16"), ("DS", 644, "bfloat16"), ("CP", 768, "bfloat16"),
-                   ("SEG", 384, "float32"), ("FF", 512, "float32"), ("CC", 384, "float32"), ("EE", 768, "float32"),
-                   ("EV", 768, "float32"), ("JK", 768, "float32"), ("TT", 384, "float32"), ("UU", 384, "float32"),
-                   ("IS", 256, "float32"), ("IB", 640, "bfloat16"), ("NU", 128, "uint16"), ("NBI", 128, "int32"),
-                   ("VI", 128, "int32")):
+                   ("DE", 384, "float32"), ("TRI", 128, "bfloat16"), ("TB", 4, "bfloat16"), ("IR2", 128, "bfloat16"),
+                   ("ST", 762, "float32"), ("EE", 768, "bfloat16"), ("AB", 768, "bfloat16"), ("CP", 768, "bfloat16"),
+                   ("CG", 384, "bfloat16"), ("DB", 272, "bfloat16"), ("HL", 272, "int32"),
+                   ("GG", 640, "bfloat16"), ("FF", 512, "float32"), ("CC", 384, "bfloat16"),
+                   ("IS", 256, "bfloat16"), ("IB", 384, "bfloat16"), ("NU", 128, "uint16"), ("NBI", 128, "int32")):
     SCRATCH[_n] = ("sbuf", [128, _w], _d)
 for _k in range(8):
     SCRATCH["P%d" % _k] = ("psum", [128, 512], "float32")
 PACK = {}
 for _b, _d, _l in (("PU", "uint16", "OFP 6 CU 6 AU 6 CL 24"),
-                   ("PN", "int32", "CI 6 C2 6 A2 6 PI 1 PC 8 OWN 128 LO 128 HI 128 OI 6 OJ 6 TI 128 VR 128 VS 128 "
-                    "GI 128 SA 128 SB 128 TJ 128 TK 128"),
+                   ("PN", "int32", "CI 6 C2 6 A2 6 PI 1 PC 8 OWN 128 OI 6 OJ 6 TI 128 VR 128 VS 128 TJ 128 TK 128"),
                    ("PX", "float32", "NB 96 NM 96 CA 24 CM 24 CY 24 CZ 24 CO 24 PF 8 KM 8 KC 1 KC2 1 RC 1 SC2 1 "
-                    "M2 2 M4 4 MJ 4 SCOL 2 VC 6 RW 12 BC 3 R1 128 R4 128 R5 128 R6 128 R7 128 TAB 128 TAR 128 LV 128 LT 128 "
-                    "LD 128 LE 128")):
+                    "M4 4 MJ 4 SCOL 2 BC 3 KI 3 HN 3 HR 3 MID 3 UA 256 LV 128 LR 128 TAR 128")):
     _l, _o = _l.split(), 0
     for _k in range(0, len(_l), 2):
         PACK[_l[_k]] = (_b, _o, int(_l[_k + 1]))
         _o += (int(_l[_k + 1]) + 7) // 8 * 8
     SCRATCH[_b] = ("sbuf", [128, _o], _d)
-SEMAPHORES = ("v s p gi ls lx dn dx dz do dw0 dw1 dw2 dy ax at an aq rq ar0 ar1 ar2".split()
+SEMAPHORES = ("v s p gi ls lx dn dx dz do dw0 dw1 dw2 dy ax an aq rq ar0 ar1 ar2".split()
               + ["ay%d%d" % (m, c) for m in range(8) for c in range(2)])
 BIG = 9.99e29
 
@@ -93,8 +93,7 @@ def team_program(g, core, T, topo, teams, r, m):
     en_hi = [b for b in en_on if b not in en_off]
     own_chip = [c for c in team if c != core and near(c, core)]
     off_chip = [c for c in team if not near(c, core)]
-    A, S = AluOpType, T.sem
-    COPY = ActivationFunctionType.Copy
+    A, S, F = AluOpType, T.sem, ActivationFunctionType
     queue = {"v": g.vector, "s": g.scalar, "p": g.tensor, "g": g, "y": g.sync}
     n, seen = {}, {}
 
@@ -121,12 +120,10 @@ def team_program(g, core, T, topo, teams, r, m):
     ts, tt, cp, fill = g.vector.tensor_scalar, g.vector.tensor_tensor, g.vector.tensor_copy, g.vector.memset
     scan = g.vector.tensor_tensor_scan
 
-    def act(out, in_, acc=None, free=False):
+    def act(out, in_, free=False):
         if not free:
             wait("s", "s")
-        if acc is None:
-            return inc(g.scalar.activation(out, in_, COPY), "s", 1)
-        return inc(g.scalar.activation(out, in_, COPY, accum_out=acc), "s", 1)
+        return inc(g.scalar.activation(out, in_, F.Copy), "s", 1)
 
     def mm(out, l, rh, st=True, sp=True):
         return inc(g.tensor.matmul(out, l, rh, st, sp), "p", 1)
@@ -136,8 +133,8 @@ def team_program(g, core, T, topo, teams, r, m):
             return inc(g.iota(out, pat, base, cm), "gi", 1)
         return inc(g.iota(out, pat, base, cm, allow_small_or_imprecise_dtypes=True), "gi", 1)
 
-    def rotate(W, c0, c1, sem):
-        for k in range(1, 8):
+    def rotate(W, c0, c1, sem, ks=range(1, 8)):
+        for k in ks:
             a = 16 * k
             inc(g.sync.dma_start(W[0:128 - a, 512 * k + c0:512 * k + c1], W[a:128, c0:c1]), sem, 16)
             inc(g.sync.dma_start(W[128 - a:128, 512 * k + c0:512 * k + c1], W[0:a, c0:c1]), sem, 16)
@@ -153,61 +150,70 @@ def team_program(g, core, T, topo, teams, r, m):
 
     W = [T.W0, T.W1, T.W2, T.R3]
     PS = [T["P%d" % k] for k in range(8)]
+    busy = {}
+
+    def bank(b):
+        if b in busy:
+            wait("p", *busy[b])
+        return PS[b]
     if isr:
         inc(g.sync.dma_start(T.NBI[:], T.nb[:]), "dn", 16)
         zf = team.index(off_chip[0])
-        for z, sem in ((zf, "dx"), (4 - zf, "dz")):
+        for z, sem in ((4 - zf, "dz"), (zf, "dx")):
             for b in range(8):
                 inc(g.sync.dma_start(T.xs[z:z + 4, 16 * b:16 * b + 16, :], T.x[16 * z:16 * z + 64, 512 * b:512 * b + 512]), sem, 16)
         for b in range(8):
             inc(g.scalar.dma_start(T.W0[16 * b:16 * b + 16, 0:512], T.x[16 * m:16 * m + 16, 512 * b:512 * b + 512]), "do", 16)
-    IR, ROWM, ROW8, ROWG = [T.IB[:, a:a + 128] for a in (0, 256, 384, 512)]
+    IR = T.IR2[:]
+    ROWM, ROW8, ROWG = [T.IB[:, a:a + 128] for a in (0, 128, 256)]
     iota(u("PI"), [[0, 1]], 0, 1, True)
-    gc0 = iota(T.IB[:, 0:256], [[0, 2], [1, 128]])
-    iota(T.IS[:], [[1, 256]])
-    iota(ROWM, [[0, 8], [1, 16]])
-    iota(ROW8, [[1, 8], [8, 16]])
-    gc1 = iota(ROWG, [[1, 8], [0, 16]])
-    gc2 = n["gi"]
-    if not isr:
-        gc2 = iota(T.DG[:], [[0, 24], [1, 16]])
+    gc0 = iota(T.IR2[:], [[1, 128]])
+    gcs = iota(T.IS[:], [[128, 2], [1, 8], [8, 16]], 1) if isr else gc0
+
+    def late_iotas():
+        iota(ROWM, [[0, 8], [1, 16]])
+        iota(ROW8, [[1, 8], [8, 16]])
+        iota(ROWG, [[1, 8], [0, 16]])
+
+    def dg_iota():
+        return iota(T.DG[:], [[0, 24], [1, 16]])
+
     pf = lambda c: u("PF", c, c + 1)
+    V(fill, T.GG[:, 0:128], 1.0, free=True)
+    V(fill, T.GG[:, 512:640], 0.0, free=True)
+    for i in range(3):
+        V(fill, u("KI", i, i + 1), 4095.0 + 256 * i, free=True)
+    if isr:
+        V(fill, T.HL[:, 128:136], 0, free=True)
+        V(fill, T.HL[:, 264:272], 0, free=True)
     wait("v", "gi", gc0)
     for c, (sh, am) in enumerate([(4, 7), (0, 15), (0, 3), (5, 3), (4, 1), (0, 127), (0, 7), (2, 3)]):
-        V(ts, u("PC", c, c + 1), u("PI"), sh, am, A.logical_shift_right, A.bitwise_and, free=c > 0)
+        V(ts, u("PC", c, c + 1), u("PI"), sh, am, A.logical_shift_right, A.bitwise_and, free=True)
     V(cp, u("PF"), u("PC"))
-    V(ts, T.TRI[:], IR, pf(5), None, A.is_gt)
-    V(fill, T.SEG[:], 1.0, free=True)
+    V(ts, T.TRI[:], T.IR2[:], pf(5), None, A.is_gt)
+    V(ts, u("RC"), pf(6), -512.0, 4096.0, A.mult, A.add, free=True)
     if isr:
-        V(ts, T.SH[:], IR, -1.0, pf(5), A.add, A.is_equal, free=True)
-        V(ts, T.CP[:, 0:128], IR, pf(5), None, A.is_equal, free=True)
-        V(tt, T.DM[:], T.CP[:, 0:128], T.SH[:], A.subtract)
-    V(fill, T.SEG[:, 0:384:128], 0.0)
-
-    def request_constants():
-        V(ts, u("SCOL", 0, 1), pf(5), 1.0, None, A.add, free=True)
-        V(ts, u("SCOL", 1, 2), pf(5), 129.0, None, A.add, free=True)
-        V(ts, u("SC2"), pf(3), 16.0, pf(1), A.mult, A.add, free=True)
-        V(ts, u("M2"), T.IB[:, 0:2], pf(4), None, A.is_equal, free=True)
+        V(ts, u("SC2"), pf(1), 8.0, pf(0), A.mult, A.add, free=True)
         V(ts, u("KC2"), pf(0), -512.0, 4096.0, A.mult, A.add, free=True)
-        wait("v", "gi", gc1)
-        V(ts, T.LL[:, 0:128], IR, u("SC2"), None, A.is_equal)
-        V(ts, T.LL[:, 128:256], IR, -64.0, u("SC2"), A.add, A.is_equal, free=True)
+        V(ts, u("SCOL", 0, 1), u("SC2"), 1.0, None, A.add)
+        V(ts, u("SCOL", 1, 2), u("SC2"), 129.0, None, A.add, free=True)
 
-    def list_constants():
-        wait("v", "gi", gc1)
-        V(ts, u("RC"), pf(6), -512.0, 4096.0, A.mult, A.add, free=True)
+    def shift_constants():
+        V(ts, T.SF[:, 0:128], IR, pf(5), None, A.is_equal, free=True)
+        V(ts, T.SF[:, 128:256], IR, pf(5), None, A.is_equal, free=True)
+
+    def list_constants(gc):
+        wait("v", "gi", gc)
         V(ts, u("KC"), pf(0), 512.0, None, A.mult, free=True)
-        V(ts, u("KM"), T.IB[:, 0:8], -1.0, pf(5), A.mult, A.add, free=True)
-        V(ts, u("M4"), T.IB[:, 0:4], pf(7), None, A.is_equal, free=True)
-        V(ts, u("MJ"), T.IB[:, 0:4], pf(2), None, A.is_equal, free=True)
+        V(ts, u("KM"), IR[:, 0:8], -1.0, pf(5), A.mult, A.add, free=True)
+        V(ts, u("M4"), IR[:, 0:4], pf(7), None, A.is_equal, free=True)
+        V(ts, u("MJ"), IR[:, 0:4], pf(2), None, A.is_equal, free=True)
         V(ts, T.S2[:], ROW8, pf(5), None, A.is_equal, free=True)
         wait("v", "v")
         for k in range(8):
             V(ts, T.S8[:, 128 * k:128 * k + 128], ROWM, 8.0, u("KM", k, k + 1), A.mult, A.is_equal, free=True)
 
     def sweep_constants():
-        wait("v", "gi", gc2)
         V(ts, T.DI[:], T.DG[:], pf(1), None, A.is_equal, free=True)
         V(fill, T.RM[:], 1.0, free=True)
         for j in range(4):
@@ -217,9 +223,17 @@ def team_program(g, core, T, topo, teams, r, m):
             V(ts, T.RB[:, 128 * b:128 * b + 128], ROWM, 16.0 * b, pf(5), A.add, A.is_equal, free=True)
         for b, c in ((T.MM[:], BIG), (T.MQ[:], BIG)):
             V(fill, b, c, free=True)
-        V(ts, T.SF[:], T.IB[:, 0:256], pf(5), None, A.is_equal, free=True)
         V(fill, T.MM[:, 0:1024:4], -BIG)
         V(fill, T.MQ[:, 0:480:5], -BIG, free=True)
+
+    def turn(sem, shifts, banks):
+        wait("p", sem)
+        wait("p", "v")
+        for x, q in enumerate(shifts):
+            b = banks[x % len(banks)]
+            px = mm(bank(b)[:], T.SF[:, 16 * q:16 * q + 128], T.W0[:, 0:512])
+            wait("s", "p", px)
+            busy[b] = ("s", act(T.W0[:, 512 * q:512 * q + 512], PS[b][:], free=True))
 
     def by_team(src, to, sem):
         ps = []
@@ -232,160 +246,150 @@ def team_program(g, core, T, topo, teams, r, m):
         by_team(lambda o: src, lambda o: T.LQ[:, 12 * others(o).index(r):12 * others(o).index(r) + 12], "aq")
 
     def number():
-        V(ts, u("OWN"), T.NBI[:], 12, None, A.logical_shift_right)
-        V(ts, T.VI[:], T.NBI[:], 4095, None, A.bitwise_and, free=True)
-        for i, o in enumerate(oth + [r]):
-            V(ts, T.FF[:, 128 * i:128 * i + 128], u("OWN"), float(o), None, A.is_equal, free=i > 0)
-        V(scan, T.CC[:], T.SEG[:], T.FF[:, 0:384], 0.0, A.mult, A.add)
+        for o in range(1, 4):
+            V(ts, T.GG[:, 128 * o:128 * o + 128], T.NU[:], 4096.0 * o, None, A.is_ge, free=o > 1)
+        wait("v", "v")
+        for i, o in enumerate(oth):
+            V(scan, T.CC[:, 128 * i:128 * i + 128], T.GG[:, 128 * o:128 * o + 128], T.GG[:, 128 * o + 128:128 * o + 256], 0.0,
+              A.add, A.subtract, free=True)
         vt = V(cp, T.TB[:, 0:3], T.CC[:, 127:384:128])
         wait("p", "v", vt)
-        pbase = mm(PS[3][:, 0:3], T.TRI[:], T.TB[:, 0:3])
-        V(tt, T.RT[:, 0:384], T.CC[:], T.FF[:, 0:384], A.mult)
-        return pbase
+        return mm(PS[3][:, 0:3], T.TRI[:], T.TB[:, 0:3])
 
-    def codes():
+    def own_codes():
+        V(ts, u("OWN"), T.NBI[:], 12, None, A.logical_shift_right)
+        V(ts, u("VS"), T.NU[:], u("RC"), None, A.add, free=True)
+        V(ts, PS[1][:, 384:512], T.NU[:], -4096.0 * r, None, A.add, free=True)
+        wait("v", "v")
+        for i, o in enumerate([r] + oth):
+            c = (i + 3) % 4 * 128
+            V(ts, T.FF[:, c:c + 128], u("OWN"), float(o), None, A.is_equal, free=True)
+        V(ts, u("VR"), u("VS"), 4095, None, A.bitwise_and, free=True)
+        V(tt, u("LV"), T.FF[:, 384:512], PS[1][:, 384:512], A.mult)
+        return V(tt, u("LR"), T.FF[:, 384:512], u("VR"), A.mult, free=True)
+
+    def columns():
+        vbc = V(tt, u("BC"), PS[3][:, 0:3], u("KI"), A.add)
+        wait("s", "v", vbc)
         for i in range(3):
-            V(ts, u("BC", i, i + 1), PS[3][:, i:i + 1], 4095.0 + 256 * i, None, A.add, free=i > 0)
-        for i in range(3):
-            c = slice(128 * i, 128 * i + 128)
-            V(ts, T.TT[:, c], T.FF[:, c], u("BC", i, i + 1), None, A.mult, free=i > 0)
-        V(tt, u("LV"), T.FF[:, 384:512], T.VI[:], A.mult, free=True)
-        V(tt, T.UU[:], T.TT[:], T.RT[:, 0:384], A.add)
-        V(tt, u("R1"), T.UU[:, 0:128], T.UU[:, 128:256], A.add)
-        V(tt, u("R4"), u("R1"), T.UU[:, 256:384], A.add)
-        V(cp, u("GI"), u("R4"))
-        V(tt, u("R5"), u("R4"), u("LV"), A.add, free=True)
-        V(ts, u("SA"), u("GI"), 224, None, A.bitwise_and)
-        V(ts, u("SB"), u("GI"), 768, None, A.bitwise_and, free=True)
-        V(ts, u("R6"), u("SA"), 2.0, None, A.mult)
-        V(ts, u("R7"), u("SB"), -0.875, None, A.mult, free=True)
-        V(tt, u("R1"), u("R5"), u("R6"), A.add)
-        V(tt, u("R6"), u("R1"), u("R7"), A.add)
-        return V(cp, T.TU[:], u("R6"))
+            sk = inc(g.scalar.activation(PS[0][:, 128 * i:128 * i + 128], T.CC[:, 128 * i:128 * i + 128], F.Identity,
+                                         u("BC", i, i + 1)), "s", 1)
+        return sk
+
+    def codes(sk):
+        wait("v", "s", sk)
+        V(tt, u("UA"), T.FF[:, 0:256], PS[0][:, 0:256], A.mult)
+        V(tt, PS[2][:, 0:128], T.FF[:, 256:384], PS[0][:, 256:384], A.mult, free=True)
+        V(tt, PS[2][:, 128:256], u("UA", 0, 128), PS[2][:, 0:128], A.add)
+        V(tt, PS[2][:, 256:384], u("UA", 128, 256), PS[2][:, 128:256], A.add)
+        vr = V(tt, u("TAR"), u("LR"), PS[2][:, 256:384], A.add)
+        V(tt, u("TI"), u("LV"), PS[2][:, 256:384], A.add, free=True)
+        for x in range(3):
+            busy[x] = ("v", n["v"])
+        return vr
 
     if isr:
         wait("v", "dn")
         vnu = V(cp, T.NU[:], T.NBI[:])
         wait("g", "v", vnu)
         to_team(T.NU[:], T.NU[:], "an")
-        wait("g", "dx")
-        fused([([c], T.xs[team.index(c)], [T.W0[:, 0:512]], en_off[2 * h:2 * h + 2], "ax") for h, c in enumerate(off_chip)], "lx")
         wait("g", "dz")
         fused([([c], T.xs[team.index(c)], [T.W0[:, 0:512]], en_hi[2 * h:2 * h + 2], "ax") for h, c in enumerate(own_chip)], "lx")
-        wait("y", "do")
-        wait("y", "lx")
-        rotate(T.W0, 0, 512, "dw0")
+        late_iotas()
         pbase = number()
-        V(ts, u("HI"), T.VI[:], 4032, None, A.bitwise_and, free=True)
-        V(ts, u("LO"), T.VI[:], 63, None, A.bitwise_and, free=True)
-        V(cp, T.RT[:, 384:512], u("HI"))
-        vr = V(cp, T.RT[:, 512:640], u("LO"), free=True)
-        wait("p", "v", vr)
-        wait("p", "p")
-        mm(PS[4][:, 0:384], T.DM[:], T.RT[:, 0:384])
-        mm(PS[5][:, 0:256], T.DM[:], T.RT[:, 384:640])
-        pd = mm(PS[5][:, 256:259], T.SH[:], T.TB[:, 0:3])
-        wait("s", "p", pd)
-        act(T.DS[:, 0:384], PS[4][:, 0:384])
-        sd = act(T.DS[:, 384:643], PS[5][:, 0:259], free=True)
+        V(ts, u("HN"), T.TB[:, 0:3], -0.5, -0.5, A.mult, A.add)
+        V(ts, u("HR"), T.TB[:, 0:3], 0.5, None, A.mult, free=True)
+        V(ts, T.HL[:, 0:128], T.NBI[:], 4032, None, A.bitwise_and, free=True)
+        V(ts, T.HL[:, 136:264], T.NBI[:], 63, None, A.bitwise_and, free=True)
         wait("v", "p", pbase)
-        wait("v", "gi", gc1)
+        vmid = V(tt, u("MID"), u("HN"), PS[3][:, 0:3], A.subtract)
+        wait("s", "gi", gcs)
+        wait("s", "v", vmid)
+        sab = [inc(g.scalar.activation(T.AB[:, 256 * i:256 * i + 256], T.IS[:], F.Abs, u("MID", i, i + 1)), "s", 1) for i in range(3)]
         for i in range(3):
-            vcp = V(ts, T.CP[:, 256 * i:256 * i + 256], T.IS[:], PS[3][:, i:i + 1], None, A.is_ge, free=i > 0)
-        request_constants()
-        wait("p", "v", vcp)
-        wait("p", "s", sd)
-        vev, ptl = {}, {}
-
-        def tile(t):
-            i, X, l = t // 2, PS[t % 3], T.CP[:, 128 * t:128 * t + 128]
-            wait("p", "p")
-            if t >= 3:
-                wait("p", "v", vev[t - 3])
-            mm(X[:, 0:128], l, T.DS[:, 128 * i:128 * i + 128])
-            mm(X[:, 128:256], l, T.DS[:, 384:512], True, False)
-            mm(X[:, 128:256], l, T.DS[:, 512:640], False, True)
-            ptl[t] = mm(X[:, 256:257], l, T.DS[:, 640 + i:641 + i])
-
-        for t in range(3):
-            tile(t)
+            V(ts, T.CG[:, 128 * i:128 * i + 128], T.CC[:, 128 * i:128 * i + 128], PS[3][:, i:i + 1], None, A.add, free=True)
+        V(tt, T.DB[:, 0:128], T.HL[:, 0:128], T.HL[:, 1:129], A.subtract, free=True)
+        V(tt, T.DB[:, 128:256], T.HL[:, 136:264], T.HL[:, 137:265], A.subtract, free=True)
+        ptl = []
+        for i in range(3):
+            wait("v", "s", sab[i])
+            vcp = V(ts, T.CP[:, 256 * i:256 * i + 256], T.AB[:, 256 * i:256 * i + 256], u("HR", i, i + 1), None, A.is_lt, free=True)
+            wait("p", "v", vcp)
+            for h in range(2):
+                X, l = PS[(0, 1, 2, 4, 5, 6)[2 * i + h]], T.CP[:, 256 * i + 128 * h:256 * i + 128 * h + 128]
+                mm(X[:, 0:128], l, T.CG[:, 128 * i:128 * i + 128])
+                mm(X[:, 128:256], l, T.DB[:, 0:128], True, False)
+                ptl.append(mm(X[:, 128:256], l, T.DB[:, 128:256], False, True))
         for t in range(6):
-            X, c = PS[t % 3], slice(128 * t, 128 * t + 128)
+            X, c = PS[(0, 1, 2, 4, 5, 6)[t]], 127 * t
             wait("v", "p", ptl[t])
-            V(ts, T.EE[:, c], X[:, 0:128], X[:, 256:257], u("SCOL", t % 2, t % 2 + 1), A.add, A.is_equal)
-            vev[t] = V(tt, T.EV[:, c], T.EE[:, c], X[:, 128:256], A.mult)
-            if t + 3 < 6:
-                tile(t + 3)
-            wait("s", "v", vev[t])
-            sacc = act(T.JK[:, c], T.EV[:, c], u("VC", t, t + 1), free=True)
-        wait("v", "s", sacc)
-        for t in range(6):
-            a = 6 * (t % 2) + 2 * (t // 2)
-            vw = V(ts, u("RW", a, a + 2), u("M2"), u("VC", t, t + 1), None, A.mult, free=t > 0)
-        wait("p", "v", vw)
-        mm(PS[6][:, 0:6], T.LL[:, 0:128], u("RW", 0, 6), True, False)
-        pw = mm(PS[6][:, 0:6], T.LL[:, 128:256], u("RW", 6, 12), False, True)
-        wait("v", "p", pw)
-        V(ts, u("OI"), PS[6][:, 0:6], u("KC2"), None, A.add)
-        V(cp, T.PB[:, 6:12], PS[6][:, 0:6], free=True)
+            V(ts, T.EE[:, 128 * t:128 * t + 127], X[:, 0:127], u("SCOL", t % 2, t % 2 + 1), None, A.is_ge, free=True)
+            V(scan, T.ST[:, c:c + 127], T.EE[:, 128 * t:128 * t + 127], X[:, 129:256], X[:, 128:129], A.mult, A.add)
+        V(ts, u("OI"), T.ST[:, 126:762:127], u("KC2"), None, A.add)
+        V(cp, T.PB[:, 6:12], T.ST[:, 126:762:127], free=True)
         V(ts, u("OJ"), u("OI"), 4095, None, A.bitwise_and)
         vpb = V(cp, T.PB[:, 0:6], u("OJ"))
         wait("g", "v", vpb)
         to_team(T.PB[:], T.FP[:], "rq")
+        wait("g", "dx")
+        fused([([c], T.xs[team.index(c)], [T.W0[:, 0:512]], en_off[2 * h:2 * h + 2], "ax") for h, c in enumerate(off_chip)], "lx")
         forward(T.PB[:])
-        gc2 = iota(T.DG[:], [[0, 24], [1, 16]])
-        n["aq"], n["at"] = 12, len(en_on)
-        list_constants()
-        sweep_constants()
-        wait("v", "at")
+        shift_constants()
+        gl = dg_iota()
+        n["aq"] = 12
+        sk = columns()
+        turn("do", BYDMA + BYPE, (4, 5, 6, 7))
+        own_codes()
+        vtr = codes(sk)
+        list_constants(gl)
     else:
         n["ax"], n["rq"], n["aq"], n["an"] = 2, 8, 12, 8
+        late_iotas()
+        gl = dg_iota()
         wait("y", "ax")
-        rotate(T.W0, 0, 512, "dw0")
-        list_constants()
+        rotate(T.W0, 0, 512, "dw0", BYDMA)
+        list_constants(gl)
+        shift_constants()
         sweep_constants()
         wait("v", "an")
-        V(cp, T.NBI[:], T.NU[:])
-        wait("v", "v")
+        V(cp, T.NBI[:], T.NU[:], free=True)
         pbase = number()
+        own_codes()
         wait("v", "p", pbase)
-        vtu = codes()
-        if core == [c for c in team if c != home and near(c, home)][0]:
-            wait("g", "v", vtu)
-            rid, pid = topo.addr(home, core)
-            g.remote_dma(T.TU[:], T.TU[:], S["at"], S["ls"], pid, rid, topo.mask(core, home))
-            n["ls"] = n.get("ls", 0) + len(en_on)
+        sk = columns()
+        vtr = codes(sk)
         wait("g", "rq")
         forward(T.FP[:])
-    V(cp, u("TI"), T.TU[:])
-    V(cp, u("TAB"), T.TU[:], free=True)
-    V(ts, u("VS"), u("TI"), u("RC"), None, A.add)
-    V(ts, u("LT"), u("TAB"), 4096.0, None, A.is_lt, free=True)
-    V(ts, u("VR"), u("VS"), 4095, None, A.bitwise_and)
-    V(ts, u("TJ"), u("TI"), 8128, None, A.bitwise_and, free=True)
-    V(tt, u("LD"), u("VR"), u("TAB"), A.subtract)
+    wait("p", "v", vtr if not isr else None)
+    pl = mm(bank(6)[:, 0:128], T.S2[:], u("TAR"))
+    V(ts, u("TJ"), u("TI"), 8128, None, A.bitwise_and)
     V(ts, u("TK"), u("TI"), 63, None, A.bitwise_and, free=True)
-    V(tt, u("LE"), u("LD"), u("LT"), A.mult)
-    vtr = V(tt, u("TAR"), u("LE"), u("TAB"), A.add)
-    wait("p", "v", vtr)
-    wait("p", "s")
-    wait("p", "p")
-    pl = mm(PS[6][:, 0:128], T.S2[:], u("TAR"))
-    V(cp, T.TH[:, 0:128], u("TJ"), free=True)
+    V(cp, T.TH[:, 0:128], u("TJ"))
     vth = V(cp, T.TH[:, 128:256], u("TK"), free=True)
     wait("p", "v", vth)
     ptg = []
     for k in range(8):
-        o = PS[4 + k // 4][:, 128 * (k % 4):128 * (k % 4) + 128]
+        o = bank(4 + k // 4)[:, 128 * (k % 4):128 * (k % 4) + 128]
         mm(o, T.S8[:, 128 * k:128 * k + 128], T.TH[:, 0:128], True, False)
         ptg.append(mm(o, T.S8[:, 128 * k:128 * k + 128], T.TH[:, 128:256], False, True))
+    if isr:
+        sweep_constants()
+    wait("v", "p", pl)
+    vlm = V(cp, T.LM[:], PS[6][:, 0:128])
+    busy[6] = ("v", vlm)
+    if not isr:
+        turn("ax", BYPE, (3, 7, 1, 0))
     cols = [12 * ri + 2 * others(o).index(r) for ri, o in enumerate(oth)]
     src = "do" if isr else "ax"
-    wait("s", "aq")
-    wait("s", "dw0")
-    wait("s", src)
-    for ri in range(3):
-        sq = act(T.QS[:, 32 * ri:32 * ri + 32], T.W0[:, 0:4096].indirect(T.LQ[:, cols[ri]:cols[ri] + 2]), free=True)
+
+    def asked0():
+        wait("s", "aq")
+        wait("s", "dw0")
+        wait("s", src)
+        wait("s", "s")
+        for ri in range(3):
+            sq = act(T.QS[:, 32 * ri:32 * ri + 32], T.W0[:, 0:4096].indirect(T.LQ[:, cols[ri]:cols[ri] + 2]), free=True)
+        return sq
 
     def send(k, sem, val):
         wait("g", sem, val)
@@ -395,13 +399,12 @@ def team_program(g, core, T, topo, teams, r, m):
             return T.RL[:, c:c + 32]
         by_team(lambda o: T.QS[:, 96 * k + 32 * oth.index(o):96 * k + 32 * oth.index(o) + 32], at, "ar%d" % k)
 
+    sq = asked0()
     send(0, "s", sq)
-    wait("v", "p", pl)
-    vlm = V(cp, T.LM[:], PS[6][:, 0:128])
     wait("v", "p", ptg[3])
-    V(cp, T.TG[:, 0:512], PS[4][:], free=True)
+    busy[4] = ("v", V(cp, T.TG[:, 0:512], PS[4][:], free=True))
     wait("v", "p", ptg[7])
-    V(cp, T.TG[:, 512:1024], PS[5][:], free=True)
+    busy[5] = ("v", V(cp, T.TG[:, 512:1024], PS[5][:], free=True))
     wait("v", "aq")
     for ri in range(3):
         V(cp, u("CI", 2 * ri, 2 * ri + 2), T.LQ[:, cols[ri] + 6:cols[ri] + 8], free=True)
@@ -413,9 +416,8 @@ def team_program(g, core, T, topo, teams, r, m):
     V(cp, u("NB"), T.TG[:].indirect(u("CU")))
     vnm = V(tt, u("NM"), u("M4").indirect(u("AU")), u("NB"), A.mult)
     wait("p", "v", vnm)
-    wait("p", "p")
     for j in range(4):
-        po = mm(PS[7][:, 96 * j:96 * j + 96], T.BD[:, 128 * j:128 * j + 128], u("NM"))
+        po = mm(bank(7)[:, 96 * j:96 * j + 96], T.BD[:, 128 * j:128 * j + 128], u("NM"))
     wait("v", "p", po)
     vdd = V(tt, T.DD[:], T.DI[:], PS[7][:, 0:384], A.mult)
     V(scan, T.DE[:], T.RM[:], T.DD[:], 0.0, A.mult, A.add)
@@ -426,99 +428,106 @@ def team_program(g, core, T, topo, teams, r, m):
     V(tt, u("CO"), u("CY"), u("CZ"), A.add)
     V(cp, u("CL"), u("CO"))
     own = PS[7]
+    busy[7] = ("v", vdd)
 
-    def spread(k):
+    def spread(k, w, who):
         n["ar%d" % k] = 12
         wait("p", "ar%d" % k)
-        for b in range(8):
-            c = 96 * b if b < 5 else 96 * (b - 5)
-            pr = mm(PS[4 + b // 5][:, c:c + 96], T.RB[:, 128 * b:128 * b + 128], T.RL[:, 96 * k:96 * k + 96])
-        return pr
+        for x, bs in enumerate(((0, 1, 2), (3, 4, 5), (6, 7))):
+            B = bank(4 + x)
+            for c, b in enumerate(bs):
+                pr = mm(B[:, 96 * c:96 * c + 96], T.RB[:, 128 * b:128 * b + 128], T.RL[:, 96 * k:96 * k + 96])
+            wait(who[x], "p", pr)
+            for c, b in enumerate(bs):
+                o = w[:, 4096 + b:4864:8]
+                z = V(cp, o, B[:, 96 * c:96 * c + 96], free=True) if who[x] == "v" else act(o, B[:, 96 * c:96 * c + 96], free=True)
+            busy[4 + x] = (who[x], z)
 
+    shift = [0]
     for k in range(3):
         w, nxt, cuts, done = W[k], W[k + 1], CUTS[k], {}
-
-        def main():
-            for c in range(1 if k else 0, len(cuts) - 1):
-                a, b = cuts[c], cuts[c + 1]
-                done[c] = act(T.GA[:, 4 * a:4 * b], w[:, 0:NW].indirect(T.LM[:, a // 4:b // 4]), free=True)
-
         if k == 0:
-            wait("p", "v", vdd)
             wait("p", src)
-            wait("p", "s")
-            wait("p", "p")
-            mm(own[:], T.SF[:, 0:128], w[:, 0:512])
-            wait("s", "p", spread(0))
-            act(w[:, 4096:4576], PS[4][:, 0:480])
-            act(w[:, 4576:4864], PS[5][:, 0:288], free=True)
+            spread(0, w, "vsv")
+            mm(bank(7)[:], T.SF[:, 0:128], w[:, 0:512])
+        pown = n["p"]
         for e in ("v", "s"):
             wait(e, "dw%d" % k)
             if k == 0:
                 wait(e, src)
-        wait("s", "v", vlm if k == 0 else None)
+        wait("s", "v")
         wait("v", "s")
         wait("s", "s")
         win = w[:, 0:NW]
-        if k == 0:
-            main()
+        wait("v", "v")
         if k < 2:
-            V(cp, T.GQ[:, 0:480:5], win.indirect(u("OFP")))
-            for j in range(2 if k else 4):
-                V(cp, T.GQ[:, 1 + j:480:5], win.indirect(u("CL", 6 * j, 6 * j + 6)), free=True)
-            if k:
-                for j in range(2, 4):
-                    sq = act(T.GQ[:, 1 + j:480:5], win.indirect(u("CL", 6 * j, 6 * j + 6)), free=True)
+            V(cp, T.GQ[:, 0:480:5], win.indirect(u("OFP")), free=True)
+        sq = 0
+        for op in PLAN[k].split():
+            c = int(op[-1]) if op[-1].isdigit() else 0
+            a, b = (cuts[c], cuts[c + 1]) if op[0] not in "QEY" else (0, 0)
+            if op[0] in "SV":
+                o, i_ = T.GA[:, 4 * a:4 * b], win.indirect(T.LM[:, a // 4:b // 4])
+                if op[0] == "S":
+                    done[c] = ("s", act(o, i_, free=True))
+                else:
+                    done[c] = ("v", V(cp, o, i_, free=True))
+            elif op[0] == "Q":
+                o, i_ = T.GQ[:, 1 + c:480:5], win.indirect(u("CL", 6 * c, 6 * c + 6))
+                if op[1] == "s":
+                    sq = act(o, i_, free=True)
+                else:
+                    V(cp, o, i_, free=True)
+            elif op == "E":
                 wait("v", "s", sq)
-            V(scan, T.SQ[:], T.MQ[:], T.GQ[:], 0.0, A.min, A.max)
-            vq = V(cp, T.QS[:, 96 * k + 96:96 * k + 192], T.SQ[:, 4:480:5])
-            send(k + 1, "v", vq)
-        if k:
-            main()
-            V(cp, T.GA[:, 0:4 * VN], win.indirect(T.LM[:, 0:VN // 4]))
-        for c in range(len(cuts) - 1):
-            a, b = cuts[c], cuts[c + 1]
-            if c in done:
-                wait("v", "s", done[c])
-            V(scan, T.SC[:, 4 * a:4 * b], T.MM[:, 0:4 * (b - a)], T.GA[:, 4 * a:4 * b], 0.0, A.min, A.max)
-            vm = V(tt, nxt[:, a:b], T.SC[:, 4 * a + 3:4 * b:4], own[:, a:b], A.max)
-            if k < 2 and b == DC:
-                wait("y", "v", vm)
-                rotate(nxt, 0, DC, "dw%d" % (k + 1))
-            elif k < 2 and b == 512:
-                wait("p", "v", vm)
-                e, free = 512 - DC, {}
-                for q in range(1, 8):
-                    bank = (0, 1, 2, 3, 6, 0, 1)[q - 1]
-                    if bank in free:
-                        wait("p", *free[bank])
-                    px = mm(PS[bank][:, 0:e], T.SF[:, 16 * q:16 * q + 128], nxt[:, DC:512])
-                    o = nxt[:, 512 * q + DC:512 * q + 512]
-                    wait("sv"[q % 2], "p", px)
-                    if q % 2:
-                        free[bank] = ("v", V(cp, o, PS[bank][:, 0:e], free=True))
-                    else:
-                        free[bank] = ("s", act(o, PS[bank][:, 0:e], free=True))
-                mm(own[:], T.SF[:, 0:128], nxt[:, 0:512])
-                pr = spread(k + 1)
-                wait("v", "p", pr)
-                wait("s", "p", pr)
-                V(cp, nxt[:, 4096:4576], PS[4][:, 0:480], free=True)
-                act(nxt[:, 4576:4864], PS[5][:, 0:288], free=True)
-            elif k == 2 and b in YC:
-                h = YC.index(b) - 1
+                V(scan, T.SQ[:], T.MQ[:], T.GQ[:], 0.0, A.min, A.max)
+                vq = V(cp, T.QS[:, 96 * k + 96:96 * k + 192], T.SQ[:, 4:480:5])
+                send(k + 1, "v", vq)
+            elif op[0] == "M":
+                wait("v", *done[c])
+                V(scan, T.SC[:, 4 * a:4 * b], T.MM[:, 0:4 * (b - a)], T.GA[:, 4 * a:4 * b], 0.0, A.min, A.max, free=True)
+                wait("v", "p", pown)
+                vm = V(tt, nxt[:, a:b], T.SC[:, 4 * a + 3:4 * b:4], own[:, a:b], A.max)
+                busy[7] = ("v", vm)
+                done[c] = vm
+            elif op[0] == "D":
+                wait("y", "v")
+                rotate(nxt, 0, b, "dw%d" % (k + 1))
+            elif op[0] == "X":
+                wait("p", "v", done[c])
+                for e, qs in (("C", (1, 2, 3)), ("c", (4, 5, 6, 7))):
+                    x = shift[0] % 4
+                    shift[0] += 1
+                    B = bank(x)
+                    for j, q in enumerate(qs):
+                        px = mm(B[:, j * (b - a):(j + 1) * (b - a)], T.SF[:, 16 * q:16 * q + 128], nxt[:, a:b])
+                    done[e, c] = (x, px, qs)
+            elif op[0] in "Cc":
+                x, px, qs = done[op[0], c]
+                e = "vs"[op[0] == "c"]
+                wait(e, "p", px)
+                for j, q in enumerate(qs):
+                    o, i_ = nxt[:, 512 * q + a:512 * q + b], PS[x][:, j * (b - a):(j + 1) * (b - a)]
+                    z = V(cp, o, i_, free=True) if e == "v" else act(o, i_, free=True)
+                busy[x] = (e, z)
+            elif op[0] == "Y":
+                h = c
+                vm = n["v"]
                 if isr:
                     e, eng = (("y", g.sync), ("s", g.scalar))[h]
                     wait(e, "v", vm)
                     for bb in range(8):
-                        inc(eng.dma_start(T.y[16 * m:16 * m + 16, 512 * bb + YC[h]:512 * bb + b],
-                                          nxt[16 * bb:16 * bb + 16, YC[h]:b]), "dy", 16)
+                        inc(eng.dma_start(T.y[16 * m:16 * m + 16, 512 * bb + YC[h]:512 * bb + YC[h + 1]],
+                                          nxt[16 * bb:16 * bb + 16, YC[h]:YC[h + 1]]), "dy", 16)
                 else:
                     wait("g", "v", vm)
                     rid, pid = topo.addr(home, core)
-                    g.remote_dma(T["Y%d" % h][m], nxt[:, YC[h]:b], S["ay%d%d" % (m, h)], S["ls"],
+                    g.remote_dma(T["Y%d" % h][m], nxt[:, YC[h]:YC[h + 1]], S["ay%d%d" % (m, h)], S["ls"],
                                  pid, rid, topo.mask(core, home))
                     n["ls"] += len(bits(topo.mask(core, home)))
+        if k < 2:
+            spread(k + 1, nxt, "vsv")
+            mm(bank(7)[:], T.SF[:, 0:128], nxt[:, 0:512])
     if isr:
         runs = [[i for i in range(8) if near(team[i], core) and i < m], [i for i in range(8) if near(team[i], core) and i > m],
                 [i for i in range(8) if not near(team[i], core)]]

from concourse.bass import DstId, RemoteDMATransfer
from concourse.mybir import AluOpType, ActivationFunctionType

NW = 4864
CUTS = ([0, 160, 240, 304, 416, 512], [0, 160, 240, 304, 416, 512], [0, 144, 256, 432, 512])
PLAN = ("Qs2 Qv0 Qs3 S0 Qv1 E V1 M1 S3 X1 S4 M0 S2 D0 M3 X3 C1 M4 c1 X4 C3 c3 c4 M2 X2 C4 C2 c2",
        "Qs2 Qv0 Qs3 S0 Qv1 E V1 M1 S3 X1 S4 M0 S2 D0 M3 X3 C1 M4 c1 X4 C3 c3 c4 M2 X2 C4 C2 c2",
        "V1 S0 S2 M1 M0 Y0 V3 M3 M2 Y1")
YC = (0, 256, 512)
BYDMA, BYPE = (1, 2, 3), (4, 5, 6, 7)
SCRATCH = {"xs": ("dram", [8, 128, 512], "bfloat16"), "Y0": ("dram", [8, 128, YC[1]], "bfloat16"),
           "Y1": ("dram", [8, 128, YC[2] - YC[1]], "bfloat16")}
for _n, _w, _d in (("W0", NW, "bfloat16"), ("W1", NW, "bfloat16"), ("W2", NW, "bfloat16"), ("R3", 512, "bfloat16"),
                   ("RL", 288, "bfloat16"), ("QS", 288, "bfloat16"),
                   ("LQ", 36, "uint16"), ("FP", 12, "uint16"), ("PB", 12, "uint16"), ("LM", 128, "uint16"),
                   ("TH", 256, "bfloat16"), ("TG", 1024, "float32"),
                   ("GA", 2048, "bfloat16"), ("SC", 2048, "bfloat16"), ("GQ", 480, "bfloat16"), ("SQ", 480, "bfloat16"),
                   ("MM", 1024, "bfloat16"), ("MQ", 480, "bfloat16"), ("S8", 1024, "bfloat16"), ("S2", 128, "float32"),
                   ("RB", 1024, "bfloat16"), ("SF", 256, "bfloat16"), ("BD", 512, "float32"),
                   ("DG", 384, "float32"), ("DI", 384, "float32"), ("RM", 384, "float32"), ("DD", 384, "float32"),
                   ("DE", 384, "float32"), ("TRI", 128, "bfloat16"), ("TB", 4, "bfloat16"), ("IR2", 128, "bfloat16"),
                   ("ST", 762, "float32"), ("EE", 768, "bfloat16"), ("AB", 768, "bfloat16"), ("CP", 768, "bfloat16"),
                   ("CG", 384, "bfloat16"), ("DB", 272, "bfloat16"), ("HL", 272, "int32"),
                   ("GG", 640, "bfloat16"), ("FF", 512, "float32"), ("CC", 384, "bfloat16"),
                   ("IS", 256, "bfloat16"), ("IB", 384, "bfloat16"), ("NU", 128, "uint16"), ("NBI", 128, "int32")):
    SCRATCH[_n] = ("sbuf", [128, _w], _d)
for _k in range(8):
    SCRATCH["P%d" % _k] = ("psum", [128, 512], "float32")
PACK = {}
for _b, _d, _l in (("PU", "uint16", "OFP 6 CU 6 AU 6 CL 24"),
                   ("PN", "int32", "CI 6 C2 6 A2 6 PI 1 PC 8 OWN 128 OI 6 OJ 6 TI 128 VR 128 VS 128 TJ 128 TK 128"),
                   ("PX", "float32", "NB 96 NM 96 CA 24 CM 24 CY 24 CZ 24 CO 24 PF 8 KM 8 KC 1 KC2 1 RC 1 SC2 1 "
                    "M4 4 MJ 4 SCOL 2 BC 3 KI 3 HN 3 HR 3 MID 3 UA 256 LV 128 LR 128 TAR 128")):
    _l, _o = _l.split(), 0
    for _k in range(0, len(_l), 2):
        PACK[_l[_k]] = (_b, _o, int(_l[_k + 1]))
        _o += (int(_l[_k + 1]) + 7) // 8 * 8
    SCRATCH[_b] = ("sbuf", [128, _o], _d)
SEMAPHORES = ("v s p gi ls lx dn dx dz do dw0 dw1 dw2 dy ax an aq rq ar0 ar1 ar2".split()
              + ["ay%d%d" % (m, c) for m in range(8) for c in range(2)])
BIG = 9.99e29


def bits(m):
    return [1 << e for e in range(16) if m >> e & 1]


def places(T, topo):
    near = lambda a, b: topo.host(a) == topo.host(b) and topo.chip(a) == topo.chip(b)
    world = range(512)
    teams = []
    for k in T.cores:
        on = [c for c in world if near(c, k) and topo.die(c) == topo.die(k)]
        here = [c for c in world if near(c, k)]
        there = [c for c in world if topo.same_plane(k, c) and topo.chip(c) == topo.chip(k)]
        off = [there[here.index(c)] for c in on]
        team = on + off
        if teams and not topo.may_write(teams[0][0], team[0]):
            team = off + on
        teams.append(team)
    return teams


def others(r):
    return [o for o in range(4) if o != r]


_cache = {}


def rank_program(g, core, T, topo):
    if "p" not in _cache:
        _cache["p"] = places(T, topo)
    teams = _cache["p"]
    for r in range(4):
        if core in teams[r]:
            return team_program(g, core, T, topo, teams, r, teams[r].index(core))


def dst(topo, d, core):
    rid, pid = topo.addr(d, core)
    return DstId(rid=rid, pnc=pid)


def team_program(g, core, T, topo, teams, r, m):
    home, team = T.cores[r], teams[r]
    isr = core == home
    oth = others(r)
    near = lambda a, b: topo.host(a) == topo.host(b) and topo.chip(a) == topo.chip(b)
    mate = [o for o in oth if near(teams[o][m], core)][0]
    far = [o for o in oth if o != mate]
    en_on, en_off = bits(topo.mask(core, teams[mate][m])), bits(topo.mask(core, teams[far[0]][m]))
    en_hi = [b for b in en_on if b not in en_off]
    own_chip = [c for c in team if c != core and near(c, core)]
    off_chip = [c for c in team if not near(c, core)]
    A, S, F = AluOpType, T.sem, ActivationFunctionType
    queue = {"v": g.vector, "s": g.scalar, "p": g.tensor, "g": g, "y": g.sync}
    n, seen = {}, {}

    def u(name, a=0, b=None, p=slice(0, 128), step=1):
        buf, o, w = PACK[name]
        return T[buf][p, o + a:o + (w if b is None else b):step]

    def wait(k, sem, val=None):
        val = n.get(sem, 0) if val is None else val
        if seen.get((k, sem), 0) < val:
            queue[k].wait_ge(S[sem], val)
            seen[(k, sem)] = val

    def inc(ins, sem, c):
        ins.then_inc(S[sem], c)
        n[sem] = n.get(sem, 0) + c
        return n[sem]

    def V(f, *a, free=False):
        if not free:
            wait("v", "v")
        return inc(f(*a), "v", 1)

    ts, tt, cp, fill = g.vector.tensor_scalar, g.vector.tensor_tensor, g.vector.tensor_copy, g.vector.memset
    scan = g.vector.tensor_tensor_scan

    def act(out, in_, free=False):
        if not free:
            wait("s", "s")
        return inc(g.scalar.activation(out, in_, F.Copy), "s", 1)

    def mm(out, l, rh, st=True, sp=True):
        return inc(g.tensor.matmul(out, l, rh, st, sp), "p", 1)

    def iota(out, pat, base=0, cm=0, ints=False):
        if ints:
            return inc(g.iota(out, pat, base, cm), "gi", 1)
        return inc(g.iota(out, pat, base, cm, allow_small_or_imprecise_dtypes=True), "gi", 1)

    def rotate(W, c0, c1, sem, ks=range(1, 8)):
        for k in ks:
            a = 16 * k
            inc(g.sync.dma_start(W[0:128 - a, 512 * k + c0:512 * k + c1], W[a:128, c0:c1]), sem, 16)
            inc(g.sync.dma_start(W[128 - a:128, 512 * k + c0:512 * k + c1], W[0:a, c0:c1]), sem, 16)

    def fused(parts, left="ls"):
        tr = [RemoteDMATransfer(dst_ids=[dst(topo, d, core) for d in ds], srcs=[src], dsts=to, dma_engine_mask=sum(e),
                                remote_sem=S[sem]) for ds, src, to, e, sem in parts]
        g.remote_dma_fused(tr, local_sem=S[left])
        n[left] = n.get(left, 0) + sum(len(p[3]) for p in parts)

    def to_team(src, to, sem):
        fused([(off_chip, src, [to for c in off_chip], en_off, sem), (own_chip, src, [to for c in own_chip], en_hi, sem)])

    W = [T.W0, T.W1, T.W2, T.R3]
    PS = [T["P%d" % k] for k in range(8)]
    busy = {}

    def bank(b):
        if b in busy:
            wait("p", *busy[b])
        return PS[b]
    if isr:
        inc(g.sync.dma_start(T.NBI[:], T.nb[:]), "dn", 16)
        zf = team.index(off_chip[0])
        for z, sem in ((4 - zf, "dz"), (zf, "dx")):
            for b in range(8):
                inc(g.sync.dma_start(T.xs[z:z + 4, 16 * b:16 * b + 16, :], T.x[16 * z:16 * z + 64, 512 * b:512 * b + 512]), sem, 16)
        for b in range(8):
            inc(g.scalar.dma_start(T.W0[16 * b:16 * b + 16, 0:512], T.x[16 * m:16 * m + 16, 512 * b:512 * b + 512]), "do", 16)
    IR = T.IR2[:]
    ROWM, ROW8, ROWG = [T.IB[:, a:a + 128] for a in (0, 128, 256)]
    iota(u("PI"), [[0, 1]], 0, 1, True)
    gc0 = iota(T.IR2[:], [[1, 128]])
    gcs = iota(T.IS[:], [[128, 2], [1, 8], [8, 16]], 1) if isr else gc0

    def late_iotas():
        iota(ROWM, [[0, 8], [1, 16]])
        iota(ROW8, [[1, 8], [8, 16]])
        iota(ROWG, [[1, 8], [0, 16]])

    def dg_iota():
        return iota(T.DG[:], [[0, 24], [1, 16]])

    pf = lambda c: u("PF", c, c + 1)
    V(fill, T.GG[:, 0:128], 1.0, free=True)
    V(fill, T.GG[:, 512:640], 0.0, free=True)
    for i in range(3):
        V(fill, u("KI", i, i + 1), 4095.0 + 256 * i, free=True)
    if isr:
        V(fill, T.HL[:, 128:136], 0, free=True)
        V(fill, T.HL[:, 264:272], 0, free=True)
    wait("v", "gi", gc0)
    for c, (sh, am) in enumerate([(4, 7), (0, 15), (0, 3), (5, 3), (4, 1), (0, 127), (0, 7), (2, 3)]):
        V(ts, u("PC", c, c + 1), u("PI"), sh, am, A.logical_shift_right, A.bitwise_and, free=True)
    V(cp, u("PF"), u("PC"))
    V(ts, T.TRI[:], T.IR2[:], pf(5), None, A.is_gt)
    V(ts, u("RC"), pf(6), -512.0, 4096.0, A.mult, A.add, free=True)
    if isr:
        V(ts, u("SC2"), pf(1), 8.0, pf(0), A.mult, A.add, free=True)
        V(ts, u("KC2"), pf(0), -512.0, 4096.0, A.mult, A.add, free=True)
        V(ts, u("SCOL", 0, 1), u("SC2"), 1.0, None, A.add)
        V(ts, u("SCOL", 1, 2), u("SC2"), 129.0, None, A.add, free=True)

    def shift_constants():
        V(ts, T.SF[:, 0:128], IR, pf(5), None, A.is_equal, free=True)
        V(ts, T.SF[:, 128:256], IR, pf(5), None, A.is_equal, free=True)

    def list_constants(gc):
        wait("v", "gi", gc)
        V(ts, u("KC"), pf(0), 512.0, None, A.mult, free=True)
        V(ts, u("KM"), IR[:, 0:8], -1.0, pf(5), A.mult, A.add, free=True)
        V(ts, u("M4"), IR[:, 0:4], pf(7), None, A.is_equal, free=True)
        V(ts, u("MJ"), IR[:, 0:4], pf(2), None, A.is_equal, free=True)
        V(ts, T.S2[:], ROW8, pf(5), None, A.is_equal, free=True)
        wait("v", "v")
        for k in range(8):
            V(ts, T.S8[:, 128 * k:128 * k + 128], ROWM, 8.0, u("KM", k, k + 1), A.mult, A.is_equal, free=True)

    def sweep_constants():
        V(ts, T.DI[:], T.DG[:], pf(1), None, A.is_equal, free=True)
        V(fill, T.RM[:], 1.0, free=True)
        for j in range(4):
            V(ts, T.BD[:, 128 * j:128 * j + 128], ROWG, pf(0), u("MJ", j, j + 1), A.is_equal, A.mult, free=j > 0)
        V(fill, T.RM[:, 0:384:16], 0.0)
        for b in range(8):
            V(ts, T.RB[:, 128 * b:128 * b + 128], ROWM, 16.0 * b, pf(5), A.add, A.is_equal, free=True)
        for b, c in ((T.MM[:], BIG), (T.MQ[:], BIG)):
            V(fill, b, c, free=True)
        V(fill, T.MM[:, 0:1024:4], -BIG)
        V(fill, T.MQ[:, 0:480:5], -BIG, free=True)

    def turn(sem, shifts, banks):
        wait("p", sem)
        wait("p", "v")
        for x, q in enumerate(shifts):
            b = banks[x % len(banks)]
            px = mm(bank(b)[:], T.SF[:, 16 * q:16 * q + 128], T.W0[:, 0:512])
            wait("s", "p", px)
            busy[b] = ("s", act(T.W0[:, 512 * q:512 * q + 512], PS[b][:], free=True))

    def by_team(src, to, sem):
        ps = []
        for h, o in enumerate([mate] + far):
            e = en_hi[0:4] if o == mate else en_off[4 * (h - 1):4 * h]
            ps.append(([teams[o][m]], src(o), [to(o)], e, sem))
        fused(ps)

    def forward(src):
        by_team(lambda o: src, lambda o: T.LQ[:, 12 * others(o).index(r):12 * others(o).index(r) + 12], "aq")

    def number():
        for o in range(1, 4):
            V(ts, T.GG[:, 128 * o:128 * o + 128], T.NU[:], 4096.0 * o, None, A.is_ge, free=o > 1)
        wait("v", "v")
        for i, o in enumerate(oth):
            V(scan, T.CC[:, 128 * i:128 * i + 128], T.GG[:, 128 * o:128 * o + 128], T.GG[:, 128 * o + 128:128 * o + 256], 0.0,
              A.add, A.subtract, free=True)
        vt = V(cp, T.TB[:, 0:3], T.CC[:, 127:384:128])
        wait("p", "v", vt)
        return mm(PS[3][:, 0:3], T.TRI[:], T.TB[:, 0:3])

    def own_codes():
        V(ts, u("OWN"), T.NBI[:], 12, None, A.logical_shift_right)
        V(ts, u("VS"), T.NU[:], u("RC"), None, A.add, free=True)
        V(ts, PS[1][:, 384:512], T.NU[:], -4096.0 * r, None, A.add, free=True)
        wait("v", "v")
        for i, o in enumerate([r] + oth):
            c = (i + 3) % 4 * 128
            V(ts, T.FF[:, c:c + 128], u("OWN"), float(o), None, A.is_equal, free=True)
        V(ts, u("VR"), u("VS"), 4095, None, A.bitwise_and, free=True)
        V(tt, u("LV"), T.FF[:, 384:512], PS[1][:, 384:512], A.mult)
        return V(tt, u("LR"), T.FF[:, 384:512], u("VR"), A.mult, free=True)

    def columns():
        vbc = V(tt, u("BC"), PS[3][:, 0:3], u("KI"), A.add)
        wait("s", "v", vbc)
        for i in range(3):
            sk = inc(g.scalar.activation(PS[0][:, 128 * i:128 * i + 128], T.CC[:, 128 * i:128 * i + 128], F.Identity,
                                         u("BC", i, i + 1)), "s", 1)
        return sk

    def codes(sk):
        wait("v", "s", sk)
        V(tt, u("UA"), T.FF[:, 0:256], PS[0][:, 0:256], A.mult)
        V(tt, PS[2][:, 0:128], T.FF[:, 256:384], PS[0][:, 256:384], A.mult, free=True)
        V(tt, PS[2][:, 128:256], u("UA", 0, 128), PS[2][:, 0:128], A.add)
        V(tt, PS[2][:, 256:384], u("UA", 128, 256), PS[2][:, 128:256], A.add)
        vr = V(tt, u("TAR"), u("LR"), PS[2][:, 256:384], A.add)
        V(tt, u("TI"), u("LV"), PS[2][:, 256:384], A.add, free=True)
        for x in range(3):
            busy[x] = ("v", n["v"])
        return vr

    if isr:
        wait("v", "dn")
        vnu = V(cp, T.NU[:], T.NBI[:])
        wait("g", "v", vnu)
        to_team(T.NU[:], T.NU[:], "an")
        wait("g", "dz")
        fused([([c], T.xs[team.index(c)], [T.W0[:, 0:512]], en_hi[2 * h:2 * h + 2], "ax") for h, c in enumerate(own_chip)], "lx")
        late_iotas()
        pbase = number()
        V(ts, u("HN"), T.TB[:, 0:3], -0.5, -0.5, A.mult, A.add)
        V(ts, u("HR"), T.TB[:, 0:3], 0.5, None, A.mult, free=True)
        V(ts, T.HL[:, 0:128], T.NBI[:], 4032, None, A.bitwise_and, free=True)
        V(ts, T.HL[:, 136:264], T.NBI[:], 63, None, A.bitwise_and, free=True)
        wait("v", "p", pbase)
        vmid = V(tt, u("MID"), u("HN"), PS[3][:, 0:3], A.subtract)
        wait("s", "gi", gcs)
        wait("s", "v", vmid)
        sab = [inc(g.scalar.activation(T.AB[:, 256 * i:256 * i + 256], T.IS[:], F.Abs, u("MID", i, i + 1)), "s", 1) for i in range(3)]
        for i in range(3):
            V(ts, T.CG[:, 128 * i:128 * i + 128], T.CC[:, 128 * i:128 * i + 128], PS[3][:, i:i + 1], None, A.add, free=True)
        V(tt, T.DB[:, 0:128], T.HL[:, 0:128], T.HL[:, 1:129], A.subtract, free=True)
        V(tt, T.DB[:, 128:256], T.HL[:, 136:264], T.HL[:, 137:265], A.subtract, free=True)
        ptl = []
        for i in range(3):
            wait("v", "s", sab[i])
            vcp = V(ts, T.CP[:, 256 * i:256 * i + 256], T.AB[:, 256 * i:256 * i + 256], u("HR", i, i + 1), None, A.is_lt, free=True)
            wait("p", "v", vcp)
            for h in range(2):
                X, l = PS[(0, 1, 2, 4, 5, 6)[2 * i + h]], T.CP[:, 256 * i + 128 * h:256 * i + 128 * h + 128]
                mm(X[:, 0:128], l, T.CG[:, 128 * i:128 * i + 128])
                mm(X[:, 128:256], l, T.DB[:, 0:128], True, False)
                ptl.append(mm(X[:, 128:256], l, T.DB[:, 128:256], False, True))
        for t in range(6):
            X, c = PS[(0, 1, 2, 4, 5, 6)[t]], 127 * t
            wait("v", "p", ptl[t])
            V(ts, T.EE[:, 128 * t:128 * t + 127], X[:, 0:127], u("SCOL", t % 2, t % 2 + 1), None, A.is_ge, free=True)
            V(scan, T.ST[:, c:c + 127], T.EE[:, 128 * t:128 * t + 127], X[:, 129:256], X[:, 128:129], A.mult, A.add)
        V(ts, u("OI"), T.ST[:, 126:762:127], u("KC2"), None, A.add)
        V(cp, T.PB[:, 6:12], T.ST[:, 126:762:127], free=True)
        V(ts, u("OJ"), u("OI"), 4095, None, A.bitwise_and)
        vpb = V(cp, T.PB[:, 0:6], u("OJ"))
        wait("g", "v", vpb)
        to_team(T.PB[:], T.FP[:], "rq")
        wait("g", "dx")
        fused([([c], T.xs[team.index(c)], [T.W0[:, 0:512]], en_off[2 * h:2 * h + 2], "ax") for h, c in enumerate(off_chip)], "lx")
        forward(T.PB[:])
        shift_constants()
        gl = dg_iota()
        n["aq"] = 12
        sk = columns()
        turn("do", BYDMA + BYPE, (4, 5, 6, 7))
        own_codes()
        vtr = codes(sk)
        list_constants(gl)
    else:
        n["ax"], n["rq"], n["aq"], n["an"] = 2, 8, 12, 8
        late_iotas()
        gl = dg_iota()
        wait("y", "ax")
        rotate(T.W0, 0, 512, "dw0", BYDMA)
        list_constants(gl)
        shift_constants()
        sweep_constants()
        wait("v", "an")
        V(cp, T.NBI[:], T.NU[:], free=True)
        pbase = number()
        own_codes()
        wait("v", "p", pbase)
        sk = columns()
        vtr = codes(sk)
        wait("g", "rq")
        forward(T.FP[:])
    wait("p", "v", vtr if not isr else None)
    pl = mm(bank(6)[:, 0:128], T.S2[:], u("TAR"))
    V(ts, u("TJ"), u("TI"), 8128, None, A.bitwise_and)
    V(ts, u("TK"), u("TI"), 63, None, A.bitwise_and, free=True)
    V(cp, T.TH[:, 0:128], u("TJ"))
    vth = V(cp, T.TH[:, 128:256], u("TK"), free=True)
    wait("p", "v", vth)
    ptg = []
    for k in range(8):
        o = bank(4 + k // 4)[:, 128 * (k % 4):128 * (k % 4) + 128]
        mm(o, T.S8[:, 128 * k:128 * k + 128], T.TH[:, 0:128], True, False)
        ptg.append(mm(o, T.S8[:, 128 * k:128 * k + 128], T.TH[:, 128:256], False, True))
    if isr:
        sweep_constants()
    wait("v", "p", pl)
    vlm = V(cp, T.LM[:], PS[6][:, 0:128])
    busy[6] = ("v", vlm)
    if not isr:
        turn("ax", BYPE, (3, 7, 1, 0))
    cols = [12 * ri + 2 * others(o).index(r) for ri, o in enumerate(oth)]
    src = "do" if isr else "ax"

    def asked0():
        wait("s", "aq")
        wait("s", "dw0")
        wait("s", src)
        wait("s", "s")
        for ri in range(3):
            sq = act(T.QS[:, 32 * ri:32 * ri + 32], T.W0[:, 0:4096].indirect(T.LQ[:, cols[ri]:cols[ri] + 2]), free=True)
        return sq

    def send(k, sem, val):
        wait("g", sem, val)

        def at(o):
            c = 96 * k + 32 * others(o).index(r)
            return T.RL[:, c:c + 32]
        by_team(lambda o: T.QS[:, 96 * k + 32 * oth.index(o):96 * k + 32 * oth.index(o) + 32], at, "ar%d" % k)

    sq = asked0()
    send(0, "s", sq)
    wait("v", "p", ptg[3])
    busy[4] = ("v", V(cp, T.TG[:, 0:512], PS[4][:], free=True))
    wait("v", "p", ptg[7])
    busy[5] = ("v", V(cp, T.TG[:, 512:1024], PS[5][:], free=True))
    wait("v", "aq")
    for ri in range(3):
        V(cp, u("CI", 2 * ri, 2 * ri + 2), T.LQ[:, cols[ri] + 6:cols[ri] + 8], free=True)
        V(cp, u("OFP", 2 * ri, 2 * ri + 2), T.LQ[:, cols[ri]:cols[ri] + 2], free=True)
    V(ts, u("C2"), u("CI"), 2, None, A.logical_shift_right)
    V(ts, u("A2"), u("CI"), 3, None, A.bitwise_and, free=True)
    V(cp, u("CU"), u("C2"))
    V(cp, u("AU"), u("A2"), free=True)
    V(cp, u("NB"), T.TG[:].indirect(u("CU")))
    vnm = V(tt, u("NM"), u("M4").indirect(u("AU")), u("NB"), A.mult)
    wait("p", "v", vnm)
    for j in range(4):
        po = mm(bank(7)[:, 96 * j:96 * j + 96], T.BD[:, 128 * j:128 * j + 128], u("NM"))
    wait("v", "p", po)
    vdd = V(tt, T.DD[:], T.DI[:], PS[7][:, 0:384], A.mult)
    V(scan, T.DE[:], T.RM[:], T.DD[:], 0.0, A.mult, A.add)
    V(cp, u("CA"), T.DE[:, 15:384:16])
    V(ts, u("CM"), u("CA"), 4096.0, u("KC"), A.is_lt, A.mult)
    V(tt, u("CY"), u("CA"), u("CM"), A.subtract)
    V(ts, u("CZ"), u("CY"), 0.0, 4096.0, A.is_lt, A.mult)
    V(tt, u("CO"), u("CY"), u("CZ"), A.add)
    V(cp, u("CL"), u("CO"))
    own = PS[7]
    busy[7] = ("v", vdd)

    def spread(k, w, who):
        n["ar%d" % k] = 12
        wait("p", "ar%d" % k)
        for x, bs in enumerate(((0, 1, 2), (3, 4, 5), (6, 7))):
            B = bank(4 + x)
            for c, b in enumerate(bs):
                pr = mm(B[:, 96 * c:96 * c + 96], T.RB[:, 128 * b:128 * b + 128], T.RL[:, 96 * k:96 * k + 96])
            wait(who[x], "p", pr)
            for c, b in enumerate(bs):
                o = w[:, 4096 + b:4864:8]
                z = V(cp, o, B[:, 96 * c:96 * c + 96], free=True) if who[x] == "v" else act(o, B[:, 96 * c:96 * c + 96], free=True)
            busy[4 + x] = (who[x], z)

    shift = [0]
    for k in range(3):
        w, nxt, cuts, done = W[k], W[k + 1], CUTS[k], {}
        if k == 0:
            wait("p", src)
            spread(0, w, "vsv")
            mm(bank(7)[:], T.SF[:, 0:128], w[:, 0:512])
        pown = n["p"]
        for e in ("v", "s"):
            wait(e, "dw%d" % k)
            if k == 0:
                wait(e, src)
        wait("s", "v")
        wait("v", "s")
        wait("s", "s")
        win = w[:, 0:NW]
        wait("v", "v")
        if k < 2:
            V(cp, T.GQ[:, 0:480:5], win.indirect(u("OFP")), free=True)
        sq = 0
        for op in PLAN[k].split():
            c = int(op[-1]) if op[-1].isdigit() else 0
            a, b = (cuts[c], cuts[c + 1]) if op[0] not in "QEY" else (0, 0)
            if op[0] in "SV":
                o, i_ = T.GA[:, 4 * a:4 * b], win.indirect(T.LM[:, a // 4:b // 4])
                if op[0] == "S":
                    done[c] = ("s", act(o, i_, free=True))
                else:
                    done[c] = ("v", V(cp, o, i_, free=True))
            elif op[0] == "Q":
                o, i_ = T.GQ[:, 1 + c:480:5], win.indirect(u("CL", 6 * c, 6 * c + 6))
                if op[1] == "s":
                    sq = act(o, i_, free=True)
                else:
                    V(cp, o, i_, free=True)
            elif op == "E":
                wait("v", "s", sq)
                V(scan, T.SQ[:], T.MQ[:], T.GQ[:], 0.0, A.min, A.max)
                vq = V(cp, T.QS[:, 96 * k + 96:96 * k + 192], T.SQ[:, 4:480:5])
                send(k + 1, "v", vq)
            elif op[0] == "M":
                wait("v", *done[c])
                V(scan, T.SC[:, 4 * a:4 * b], T.MM[:, 0:4 * (b - a)], T.GA[:, 4 * a:4 * b], 0.0, A.min, A.max, free=True)
                wait("v", "p", pown)
                vm = V(tt, nxt[:, a:b], T.SC[:, 4 * a + 3:4 * b:4], own[:, a:b], A.max)
                busy[7] = ("v", vm)
                done[c] = vm
            elif op[0] == "D":
                wait("y", "v")
                rotate(nxt, 0, b, "dw%d" % (k + 1))
            elif op[0] == "X":
                wait("p", "v", done[c])
                for e, qs in (("C", (1, 2, 3)), ("c", (4, 5, 6, 7))):
                    x = shift[0] % 4
                    shift[0] += 1
                    B = bank(x)
                    for j, q in enumerate(qs):
                        px = mm(B[:, j * (b - a):(j + 1) * (b - a)], T.SF[:, 16 * q:16 * q + 128], nxt[:, a:b])
                    done[e, c] = (x, px, qs)
            elif op[0] in "Cc":
                x, px, qs = done[op[0], c]
                e = "vs"[op[0] == "c"]
                wait(e, "p", px)
                for j, q in enumerate(qs):
                    o, i_ = nxt[:, 512 * q + a:512 * q + b], PS[x][:, j * (b - a):(j + 1) * (b - a)]
                    z = V(cp, o, i_, free=True) if e == "v" else act(o, i_, free=True)
                busy[x] = (e, z)
            elif op[0] == "Y":
                h = c
                vm = n["v"]
                if isr:
                    e, eng = (("y", g.sync), ("s", g.scalar))[h]
                    wait(e, "v", vm)
                    for bb in range(8):
                        inc(eng.dma_start(T.y[16 * m:16 * m + 16, 512 * bb + YC[h]:512 * bb + YC[h + 1]],
                                          nxt[16 * bb:16 * bb + 16, YC[h]:YC[h + 1]]), "dy", 16)
                else:
                    wait("g", "v", vm)
                    rid, pid = topo.addr(home, core)
                    g.remote_dma(T["Y%d" % h][m], nxt[:, YC[h]:YC[h + 1]], S["ay%d%d" % (m, h)], S["ls"],
                                 pid, rid, topo.mask(core, home))
                    n["ls"] += len(bits(topo.mask(core, home)))
        if k < 2:
            spread(k + 1, nxt, "vsv")
            mm(bank(7)[:], T.SF[:, 0:128], nxt[:, 0:512])
    if isr:
        runs = [[i for i in range(8) if near(team[i], core) and i < m], [i for i in range(8) if near(team[i], core) and i > m],
                [i for i in range(8) if not near(team[i], core)]]
        for h in range(2):
            Y = T["Y%d" % h]
            for run in [x for x in runs if x]:
                for i in run:
                    n["ay%d%d" % (i, h)] = len(bits(topo.mask(team[i], core)))
                for bb in range(8):
                    e, eng = (("y", g.sync), ("s", g.scalar))[bb % 2]
                    for i in run:
                        wait(e, "ay%d%d" % (i, h))
                    inc(eng.dma_start(T.y[16 * run[0]:16 * run[-1] + 16, 512 * bb + YC[h]:512 * bb + YC[h + 1]],
                                      Y[run[0]:run[-1] + 1, 16 * bb:16 * bb + 16, :]), "dy", 16)
    for sem in n:
        wait("g", sem)
